import numpy as np, ml_dtypes
CORES = [16,18,20,22]
N = 4
BF = ml_dtypes.bfloat16
def gentries(a):
    return np.ascontiguousarray(a.reshape(8, 16, -1).transpose(0, 2, 1)).reshape(8, -1)
def gtable(e):
    e = np.asarray(e); return np.ascontiguousarray(e.reshape(8, -1, 16).transpose(0, 2, 1)).reshape(128, -1).astype(np.int32)
V, G, Q, LN, CAP, RO = 2560, 1536, 1, 256, 48, 4
W = V + Q * G
def ghosts(a):
    return np.concatenate([a] + [np.roll(a, -d, axis=0)[..., :G] for d in range(1, Q + 1)], axis=-1)
def lists(rng, cl, share):
    cw = ghosts(cl); out = np.zeros((N, 8, 16, V), np.int64)
    for a in range(N):
        for g in range(8):
            c = cw[a, g]; o = np.argsort(c + rng.random(W)); cnt = np.bincount(c); s = np.add.accumulate(cnt) - cnt; m = cl[a, g]
            y = o[s[m] + (rng.random((16, V)) * cnt[m]).astype(np.int64)]
            out[a, g] = np.where(rng.random((16, V)) < share, rng.integers(0, W, (16, V)), y)
    return out
def front(rng, x, l, share):
    xw = ghosts(x).astype(np.int16)
    for a in range(N):
        for g in range(8):
            y = l[a, g]; e = np.sum(np.abs(xw[a, g][:, y] - xw[a, g][:, None, :V]), axis=0)
            k = np.argmin(np.where(y == np.arange(V), 9999, e), axis=0); w = np.nonzero(rng.random(V) < share[a, g])[0]
            old = y[0, w].copy(); y[0, w] = y[k[w], w]; y[k[w], w] = old
    return l
def parts(rng):
    kc = W // 24; cl = rng.integers(0, kc, (N, 8, V)); cen = rng.integers(0, 256, (8, kc, 16))
    x = cen[np.arange(8)[None, :, None], cl].transpose(0, 1, 3, 2) + rng.integers(-24, 25, (N, 8, 16, V))
    return np.clip(x, 0, 255), lists(rng, cl, 0.12)
def pack(x, l, p, th):
    return {"feat": np.ascontiguousarray(x.reshape(N, 128, V)).astype(np.float32).astype(BF), "hits": np.ascontiguousarray(l.reshape(N, 128, V)).astype(np.int32),
            "lane0": np.stack([gtable(a) for a in p]), "th": np.ascontiguousarray(np.reshape(th, (N, 8, 1))).astype(np.int32)}
def setup_inputs(rng):
    x, l = parts(rng); l = front(rng, x, l, rng.choice(np.array([0.3, 0.6, 0.9]), (N, 8)))
    return pack(x, l, rng.integers(0, V, (N, 8, LN)), rng.integers(60, 400, (N, 8)))
def setup_inputs_ends(rng):
    e = np.array([0, W - 1]); x = 255 * rng.integers(0, 2, (N, 8, 16, V)); x[:, 1::2] = x[:, 1::2, :1].copy()
    x[:, 1::2, :, 0] = 0; x[:, 1::2, :, G - 1] = 0; x[:, 1::2, :, G] = 0; x[:, 1::2, :, V - 4:] = 255
    l = np.zeros((N, 8, 16, V), np.int64); p = np.zeros((N, 8, LN), np.int64); k = 3 * LN // 5 + 1; n = LN - k - 3
    for a in range(N):
        for g in range(8):
            o = np.sort(rng.permutation(np.setdiff1d(np.arange(1, V - 4), np.array([G - 1, G])))[:2 * n].reshape(n, 2), axis=1)
            v = np.append(o[:, 0], V - 2); b = np.append(o[:, 1], V - 1); xx = x[a, g]
            if g % 2 == 1: xx[:, v] = 255
            xx[:, b] = xx[:, v]
            y = np.where(rng.random((16, V)) < 0.7, rng.choice(e, (16, V)), rng.integers(0, W, (16, V)))
            y[:, v] = rng.choice(e, (16, n + 1)); y[:, b] = rng.choice(e, (16, n + 1))
            y[rng.integers(0, 15, n + 1), v] = b; y[0, b] = v; y[15, V - 2] = W - 1; y[15, V - 1] = W - 1
            y[:, V - 3] = rng.choice(e, 16); y[0, V - 3] = W - 1; y[15, V - 3] = 0
            y[:, V - 4] = W - 1; y[7, V - 4] = G; y[15, V - 4] = G - 1
            l[a, g] = y
            p[a, g] = np.concatenate([rng.permutation(np.concatenate([rng.choice(np.array([0, V - 1]), k), o[:, 0]])), np.array([V - 4, V - 3, V - 2])])
    return pack(x, l, p, np.stack([rng.permutation(np.array([0, 4080] * 4)) for a in range(N)]))
def setup_inputs_corners(rng):
    x = rng.integers(0, 256, (N, 8, 16, V)); l = np.zeros((N, 8, 16, V), np.int64); p = np.zeros((N, 8, LN), np.int64)
    half = G // 2; me = np.arange(V); p1 = LN // 2; p2 = LN // 8
    for a in range(N):
        for g in range(8):
            even = g % 2 == 0; n = int(rng.choice(np.array([0, 1, CAP - 1, CAP, CAP + 1, p1])))
            if a == 0: n = (CAP, CAP + 1, p1, CAP - 1, 1, 0, CAP, CAP + 1)[g]
            u = G + 1 + rng.permutation(V - G - 2)[:2 * p2]
            if even: u[0] = G
            u = np.sort(u)
            lo = rng.permutation(half)[:p1]; hi = rng.permutation(np.setdiff1d(np.arange(half, V - 1), np.append(u, np.array([G - 1, G]))))[:p1]
            if even:
                lo[0] = G - 1; hi[0] = V - 1
            else:
                hi[0] = G - 1; hi[1] = G
            v = np.concatenate([lo, u[0::2]]); b = np.concatenate([hi, u[1::2]])
            rest = np.setdiff1d(me, np.concatenate([v, b]))
            y = np.where(rng.random((16, V)) < 0.5, (rng.random((16, V)) * me).astype(np.int64), rng.integers(V, W, (16, V)))
            y = np.where(rng.random(V) < 0.0625, me, y)
            z = rest[rng.random(rest.size) < 0.5]; y[rng.integers(0, 8, z.size), z] = V + G - 1
            if Q > 1:
                z = rest[rng.random(rest.size) < 0.5]; y[rng.integers(8, 16, z.size), z] = V + G
            y[:, v] = rng.integers(V, W, (16, v.size)); y[:, b] = rng.integers(V, W, (16, v.size))
            r = rng.integers(0, 16, v.size)
            if even: r[0] = 1 + r[0] % 15
            y[r, v] = b; y[0, b] = v
            if even:
                y[0, v[0]] = rng.integers(0, G - 1); y[r[0], b[0]] = rng.integers(0, G - 1)
            l[a, g] = y
            xx = x[a, g]; xx[:, b] = xx[:, v]
            f = rng.integers(0, 16, v.size); s = rng.integers(2, 4, v.size); xx[f, b] += np.where(xx[f, b] < 128, s, -s)
            w = rng.choice(rest, LN - n - p2)
            if g == 7: w[:] = rest[-1]
            o = np.concatenate([lo[:n], u[0::2], w]); k = 2 if n >= 2 and not even else 0
            p[a, g] = np.concatenate([o[:k], rng.permutation(o[k:])])
    return pack(x, l, p, rng.choice(np.array([0, 1, 200, 4079, 4080]), (N, 8)))
def setup_inputs_trees(rng):
    x, l = parts(rng); p = np.zeros((N, 8, LN), np.int64); j = np.arange(16)
    th = rng.choice(np.array([0, 100, 500, 4080]), (N, 8)); th[:, 1] = rng.choice(np.array([0, 100, 500]), N)
    at = 2 * (j & 1) + 8 * ((j >> 1) & 1) + 32 * ((j >> 2) & 1) + 128 * ((j >> 3) & 1)
    for a in range(N):
        for g in (0, 1, 3, 4, 5, 7):
            n = LN // 16 if g % 2 == 0 else LN // 32; k = 8 * (g % 2); c = rng.permutation(V)
            o = np.sort(c[:16 * n].reshape(n, 16), axis=1); xx, y = x[a, g], l[a, g]
            for i in range(n):
                xx[:, o[i]] = rng.integers(0, 86, (16, 1)) + at[None, :]
                y[:, o[i]] = rng.permutation(o[i])[:, None]
            s = np.sort(c[16 * n:16 * n + 3 * k].reshape(k, 3), axis=1); u, b, w = s[:, 0], s[:, 1], s[:, 2]
            xx[:, b] = xx[:, u] ^ 128; y[:, u] = b; y[:, b] = u; y[:, w] = b
            p[a, g] = rng.permutation(np.concatenate([o.reshape(-1), b, w, rng.integers(0, V, LN - 16 * n - 2 * k)]))
    for g in (2, 6):
        th[:, g] = np.where((np.arange(N) + g // 4) % 2 == 0, 4080, rng.integers(1000, 1500, N))
        x[:, g] = rng.integers(0, 256, (N, 16, V)); pr = np.zeros((N, 2 * CAP, 2), np.int64)
        for a in range(N): pr[a] = np.sort(rng.permutation(G - 1)[:4 * CAP].reshape(2 * CAP, 2), axis=1)
        for a in range(N):
            u, b = pr[a, :, 0], pr[a, :, 1]; xx, y = x[a, g], l[a, g]
            o = rng.permutation(np.setdiff1d(np.arange(V), np.concatenate([u, b, np.array([G - 1, G])]))); w = o[:CAP]; s = o[CAP:LN - 2 * CAP]
            xx[:, b] = np.clip(xx[:, u] + rng.integers(-8, 9, (16, 2 * CAP)), 0, 255)
            y[:, u] = b; y[:, b] = rng.choice(np.array([G - 1, G]), (16, 2 * CAP)); y[0, b] = u; y[:, w] = u[:CAP]
            d = rng.integers(0, Q, (16, s.size)); m = pr[(a + 1 + d) % N, rng.integers(0, 2 * CAP, d.shape), rng.integers(0, 2, d.shape)]
            y[:, s] = V + d * G + np.where(rng.random(d.shape) < 0.75, m, rng.integers(0, G, d.shape))
            p[a, g] = rng.permutation(np.concatenate([b, w, s]))
    return pack(x, l, p, th)
def setup_inputs_ties(rng):
    x = np.full((N, 8, 16, V), 100); x[:, :, 3] += rng.integers(0, 3, (N, 8, V)); x[:, :, 12] += rng.integers(0, 3, (N, 8, V))
    x[..., :] += rng.integers(0, 156 - 2, (N, 8, 1, 1)) * rng.integers(0, 2, (N, 8, 1, V))
    l = lists(rng, rng.integers(0, W // 24, (N, 8, V)), 0.1); l[:, ::2, 8:] = l[:, ::2, :8].copy()
    l = front(rng, x, l, np.full((N, 8), 0.6))
    p = rng.integers(0, V, (N, 8, LN)); p[:, 1::4] = rng.integers(0, 64, (N, 2, LN)); p[:, 3] = V - 1 - rng.integers(0, 128, (N, LN))
    th = rng.integers(0, 5, (N, 8)); th[:, 6] = 2049 + 2 * rng.integers(0, 1016, N); th[:, 7] = rng.choice(np.array([2049, 2051, 4077, 4079]), N)
    for a in range(N):
        for g in (6, 7):
            m = 4 * rng.permutation(V // 4)[:8]; o = rng.permutation(np.setdiff1d(np.arange(V), np.concatenate([m, m + 1])))[:72]
            n = o[:32]; s = np.sort(o[32:64].reshape(16, 2), axis=1); v, b = s[:, 0], s[:, 1]; xx, y = x[a, g], l[a, g]; t = int(th[a, g])
            xx[:, o[:64]] = 0; xx[:, m] = 128; xx[:, m + 1] = 128
            xx[:, o[64:68]] = ((t + np.arange(16)) // 16)[:, None]; xx[:, o[68:72]] = ((t + 1 + np.arange(16)) // 16)[:, None]
            j = rng.integers(0, 8, 32); y[:, n] = o[64 + rng.integers(0, 8, (16, 32))]; y[0, n] = m[j] + 1; y[15, n] = m[j]
            j = rng.integers(0, 8, 16); y[:, v] = m[j] + 1; y[:, b] = m[j]; y[0, v] = b; y[0, b] = v
            p[a, g] = rng.permutation(np.concatenate([n, v, rng.integers(0, V, LN - 48)]))
    return pack(x, l, p, th)
def setup_inputs_spread(rng):
    x = np.minimum((np.exp2(8 * rng.random((N, 8, 1, V))) * rng.random((N, 8, 16, V))).astype(np.int64), 255)
    l = lists(rng, ((W // 16) * rng.random((N, 8, V)) ** 2).astype(np.int64), 0.1); l = front(rng, x, l, rng.choice(np.array([0.5, 1.0]), (N, 8)))
    return pack(x, l, (V * rng.random((N, 8, LN)) ** 1.5).astype(np.int64), (4081 * rng.random((N, 8)) ** 2).astype(np.int64))
def check_inputs(d):
    bad = []
    for k, lo, hi in (("feat", 0, 255), ("hits", 0, W - 1), ("lane0", 0, V - 1), ("th", 0, 4080)):
        v = np.asarray(d[k]).astype(np.float64)
        if not (np.min(v) >= lo and np.max(v) <= hi): bad.append("range of " + k)
        elif np.any(v != np.floor(v)): bad.append("whole numbers of " + k)
    return bad
def at_names(tab, names):
    return np.take_along_axis(tab, names.reshape(N, 8, -1), 2).reshape(names.shape)
def far(x, names, y):
    s = np.zeros(names.shape, np.int64)
    for f in range(16): s += np.abs(at_names(x[:, :, f], names) - y[:, :, f][:, :, None, :])
    return s
def reference(feat, hits, lane0, th):
    x = ghosts(feat.astype(np.float32).astype(np.int64).reshape(N, 8, 16, V)); l = ghosts(hits.astype(np.int64).reshape(N, 8, 16, V))
    t = th.astype(np.int64).reshape(N, 8, 1, 1); p = np.stack([gentries(a) for a in lane0]).astype(np.int64)
    for d in range(1, Q + 1):
        off = V + (d - 1) * G; h = l[..., off:off + G]
        l[..., off:off + G] = np.where(h < G, off + h, off + np.arange(G))
    fw = np.tile(np.arange(W), (N, 8, 1)); best = l[:, :, 0, :V].copy()
    lower = np.arange(LN)[None, :] < np.arange(LN)[:, None]
    for rnd in range(RO):
        v = p; awake = ~np.any((v[..., :, None] == v[..., None, :]) & lower, axis=3)
        v4 = v[:, :, None, :]
        c = at_names(fw, np.take_along_axis(l, v4, 3)); xv = np.take_along_axis(x, v4, 3)
        e = np.where(c == v4, 4096, far(x, c, xv))
        b = np.min(e * 4096 + c, axis=2) & 4095; b4 = b[:, :, None, :]
        a, g, i = np.nonzero(awake); best[a, g, v[a, g, i]] = b[a, g, i]
        own = b < V
        back = at_names(fw, at_names(best, np.minimum(b, V - 1)))
        join = awake & own & (b > v) & (back == v)
        o = at_names(fw, np.take_along_axis(l, b4, 3)); xn = (xv + np.take_along_axis(x, b4, 3)) >> 1
        kc = np.where((c == v4) | (c == b4), 4096 * 4096 + v4, far(x, c, xn) * 4096 + c)
        ko = np.where((o == v4) | (o == b4), 4096 * 4096 + v4, far(x, o, xn) * 4096 + o)
        nl = np.where(join[:, :, None, :], np.minimum(kc, ko) & 4095, np.where(e > t, o, c))
        ct = c[:, :, rnd]
        to = np.where(join, v, np.where(own, b, np.where(ct < V, ct, v)))
        p = np.where(awake, to, v)
        a, g, i = np.nonzero(awake)
        l[a, g, :, v[a, g, i]] = nl[a, g, :, i]
        a, g, i = np.nonzero(join); x[a, g, :, v[a, g, i]] = xn[a, g, :, i]; fw[a, g, b[a, g, i]] = v[a, g, i]
        tell = join & (v < G); cnt = np.add.accumulate(tell.astype(np.int64), axis=2); tell = tell & (cnt <= CAP)
        a, g, i = np.nonzero(tell); m = v[a, g, i]; w = b[a, g, i]; y = nl[a, g, :, i]
        for d in range(1, Q + 1):
            off = V + (d - 1) * G; q = (a - d) % N
            x[q, g, :, off + m] = xn[a, g, :, i]; l[q, g, :, off + m] = np.where(y < G, off + y, (off + m)[:, None])
            s = w < G; fw[q[s], g[s], off + w[s]] = off + m[s]
        fw = np.take_along_axis(fw, fw, 2); p = at_names(fw, p)
    return {"yx": x[..., :V].reshape(N, 128, V).astype(np.float32).astype(BF), "yl": l[..., :V].reshape(N, 128, V).astype(np.float32), "yf": fw[..., :V].astype(np.float32)}

@@ -1,0 +1,840 @@
+import numpy as np
+from concourse.mybir import AluOpType, ActivationFunctionType
+
+V, GH, WN, LN, CAP, RO = 2560, 1536, 4096, 256, 48, 4
+WD = 4416
+MARK = 4096
+ODUM = 4160
+BIG = 1048576.0
+MAGIC = 12582912.0
+SC = 33554432.0
+F32, BF, H16, I32, U16 = "float32", "bfloat16", "float16", "int32", "uint16"
+
+SCRATCH = {}
+PLACE = {}
+
+
+def _sb(dtype, size, **kw):
+    pool, at = "pool_" + dtype, 0
+    for k in kw:
+        if kw[k] > 64:
+            SCRATCH[k] = ("sbuf", [128, kw[k]], dtype)
+            PLACE[k] = (k, 0, kw[k], size)
+        else:
+            PLACE[k] = (pool, at, kw[k], size)
+            at += (kw[k] + 15) // 16 * 16
+    SCRATCH[pool] = ("sbuf", [128, at], dtype)
+
+
+_sb(F32, 4, P=WD, L=WD, Ft=WD, Pc=4096, Po=4096, YF=V, Pv0=256, Pv1=256, Pb=256, Px=256, A=256, Ao=256, sc=256, aY=256, bz=256, bR=256,
+    Ya=256, Yb=256, Yc=512, rp=256, aV=256, mv=256, t1=256, t2=256, tv=64, blkB=8, tj=32, vb0=32, vb1=32, tmp=512, tc=384, acc0=32, acc1=32,
+    bia0=32, bia1=32, vT0=32, vT1=32, aw0=16, aw1=16, sl0=16, sl1=16, tw=64, tq=64, tz=64, s1=16, l0f=16,
+    I32m=128, nsr=128, W16c=16, W16o=16, ns8=8, blk=8, mR=512, rst=256, rs8=48, Gm=48, I384=384, col=32, LNc=16, dum=32,
+    ds=8, thf=8, on32=128, lnf=16, g24=24, gs=48, gs2=48, gs3=8, gs4=8, LM0=48, LM1=48, LM2=48, DT0=304, DT1=304, DT2=304,
+    PZ0=312, PZ1=312, PZ2=312, EM0=56, EM1=56, EM2=56, LS0=48, LS1=48, LS2=48)
+_sb(BF, 2, X=WD, xm0=256, xm1=256, xb=256, zr=256, zm=256, gt=256, lt=256, mw=256, junk=4352, Ib=128, nIb=128, hIb=128, pb=128, nb=128, IO=512, WI=128,
+    Tri=128, onb=128, tl=16)
+_sb(H16, 2, Mc=4096, Mo=4096, Mz=4096, xT=256, zT=256, xo=256, p160=256, p161=256, B16=256, OH=768, Ih=128,
+    I8=128, Rep=512, b2=8, nb2=8, s0=8, Big=144, onh=128, offh=128, j5=256, ph=128, Y0=256, vq=16, bq=16, lnh=2)
+_sb(I32, 4, B=WD, NL=256, ki=256, kb=16, kc=16, bI=32, JI=256, J2=256, J3=512, pI=8, l0=16, thi=8)
+_sb(U16, 2, hc=256, ho=256, vu0=16, vu1=16, bu=16, sv0=16, sv1=16, xu=16, tu=16, ru=64, ou=24, cu0=4, cu1=4, cu2=4,
+    K0=40, K1=40, K2=40, K3=40)
+for _n in ("R0", "R1", "KZ", "M1", "M2", "W"):
+    SCRATCH[_n] = ("psum", [128, 512], F32)
+    PLACE[_n] = (_n, 0, 512, 4)
+for _n in ("KC", "KO"):
+    SCRATCH[_n] = ("psum", [128, 2, 256], F32)
+PSUM = ("R0", "R1", "KZ", "M1", "M2", "W", "KC", "KO")
+SEMAPHORES = ["eV", "eS", "eP", "eG"] + ["d%d" % i for i in range(24)] + ["r%d" % i for i in range(8)] + ["l%d" % i for i in range(8)]
+
+TM = dict(cy=1.04, g=1.56, s=3.8, pe=0.53, fix=60.0, wake=100.0, bw=200.0, dfix=2000.0, look=150.0, lam=4.0, lamc=0.5, sg=8, xa=20000.0,
+          xr=1000.0, xz=0.0, xt=0.0, k1="KC", xh=35000.0, it=30, seed=1, noise=40.0, mix=1.0)
+
+
+def rank_program(g, core, T, topo):
+    rank = T.rank_of(core)
+    if rank is None:
+        return
+    O, F = AluOpType, ActivationFunctionType
+    dst = T.cores[(rank - 1) % len(T.cores)]
+    rid, pid = topo.addr(dst)[0], topo.addr(dst)[1]
+    emask = topo.mask(core, dst)
+    neng = len(topo.engines(core, dst))
+    ops = []
+
+    def a(n, lo=0, hi=None, st=None, p=None):
+        buf, at, w, size = PLACE[n]
+        if hi is None:
+            hi = w
+        ps = slice(None) if p is None else slice(p[0], p[1])
+        return (T[buf][ps, slice(at + lo, at + hi, st)], [(n, lo, hi)], len(range(lo, hi, st or 1)), size, n in PSUM, False)
+
+    def k3(n, r, lo, hi, st=None):
+        rr = (0, 1) if r is None else (r,)
+        return (T[n][:, slice(None) if r is None else r, slice(lo, hi, st)], [(n, 256 * x + lo, 256 * x + hi) for x in rr],
+                len(rr) * len(range(lo, hi, st or 1)), 4, True, False)
+
+    def ind(w, o):
+        return (w[0].indirect(o[0]), w[1] + o[1], 16 * o[2], w[3], False, True)
+
+    def val(x):
+        return x[0] if isinstance(x, tuple) else x
+
+    def rs(*xs):
+        return [r for x in xs if isinstance(x, tuple) for r in x[1]]
+
+    def add(alts, rd, wr, kind="c", sem=None, n=1):
+        ops.append((alts, rd, wr, kind, sem, n, [0.0]))
+
+    def early(x):
+        ops[-1][6][0] = x
+
+    def tm(n, per):
+        return TM["fix"] + max(64.0, n * per) * TM["cy"]
+
+    def one(o, x):
+        return tm(o[2], TM["g"] if x[5] else 0.5 if o[3] == 2 and x[3] == 2 else 1.0)
+
+    def cp(o, i):
+        add({"V": (lambda: g.vector.tensor_copy(o[0], i[0]), one(o, i))}, i[1], o[1])
+
+    def sca(w, off, i):
+        add({"V": (lambda: g.vector.tensor_copy(w[0].indirect(off[0]), i[0]), tm(i[2], TM["s"]))}, i[1] + off[1], w[1])
+
+    def tt(o, x, y, op):
+        add({"V": (lambda: g.vector.tensor_tensor(o[0], x[0], y[0], op), tm(o[2], TM["g"] if x[5] else 1.0 if x[4] or y[4] else 2.0))},
+            x[1] + y[1], o[1])
+
+    def vts(o, x, s1, op0, s2=None, op1=None):
+        if op1 is None:
+            return (lambda: g.vector.tensor_scalar(o[0], x[0], val(s1), None, op0), one(o, x))
+        return (lambda: g.vector.tensor_scalar(o[0], x[0], val(s1), val(s2), op0, op1), one(o, x))
+
+    def ts(o, x, s1, op0, s2=None, op1=None):
+        add({"V": vts(o, x, s1, op0, s2, op1)}, rs(x, s1, s2), o[1])
+
+    def scan(o, d0, d1, init, op0, op1):
+        add({"V": (lambda: g.vector.tensor_tensor_scan(o[0], d0[0], d1[0], init, op0, op1), tm(o[2], 1.0))}, d0[1] + d1[1], o[1])
+
+    def ms(o, c):
+        add({"V": (lambda: g.vector.memset(o[0], c), one(o, o))}, [], o[1])
+
+    def sact(o, i, f, bias, scale):
+        return (lambda: g.scalar.activation(o[0], i[0], f, bias=val(bias), scale=val(scale)), tm(o[2], TM["g"] if i[5] else 1.0))
+
+    def act(o, i, f=F.Identity, bias=0.0, scale=1.0, acc=None):
+        if acc is None:
+            add({"S": sact(o, i, f, bias, scale)}, rs(i, bias, scale), o[1])
+        else:
+            add({"S": (lambda: g.scalar.activation(o[0], i[0], f, bias=val(bias), scale=val(scale), accum_out=acc[0]), tm(o[2], 1.0) + 20)},
+                rs(i, bias, scale), o[1] + acc[1])
+
+    def aff(o, x, scale=1.0, bias=0.0, more=(), lam=None):
+        add({"V": vts(o, x, scale, O.mult, bias, O.add) + (lam,), "S": sact(o, x, F.Identity, bias, scale)}, rs(x, scale, bias) + list(more), o[1])
+
+    def mm(o, l, r, st, sp):
+        add({"P": (lambda: g.tensor.matmul(o[0], l[0], r[0], st, sp), 10 + max(min(64, l[2]), r[2]) * (4 if l[3] == 4 else 1) * TM["pe"])},
+            l[1] + r[1], o[1])
+
+    def grp(items):
+        for n, (o, l, r) in enumerate(items):
+            if n == len(items) - 1:
+                o = (o[0], [x for it in items for x in it[0][1]]) + o[2:]
+            mm(o, l, r, n == 0, n == len(items) - 1)
+
+    def iota(o, pat, base, cm, fl=True):
+        if fl:
+            add({"G": (lambda: g.iota(o[0], pat, base, cm, allow_small_or_imprecise_dtypes=True), 130 + 2 * o[2] * TM["cy"])}, [], o[1])
+        else:
+            add({"G": (lambda: g.iota(o[0], pat, base, cm), 130 + 2 * o[2] * TM["cy"])}, [], o[1])
+
+    nd, nr = [0], [0]
+
+    def dma(o, i, size):
+        add({"Y": (lambda: g.sync.dma_start(o[0], i[0]), size)}, i[1], o[1], "d", "d%d" % nd[0], 16)
+        nd[0] += 1
+
+    def send(o, i, more=()):
+        n = nr[0]
+        nr[0] += 1
+        add({"G": (lambda: g.remote_dma(o[0], i[0], T.sem["r%d" % n], T.sem["l%d" % n], pid, rid, emask), 128 * i[2] * i[3])},
+            i[1] + list(more), [], "r", "l%d" % n, neng)
+        add({}, [], o[1], "a", "r%d" % n, neng)
+
+    def hb(x):
+        return (x, [])
+
+    dma(a("X", 0, GH), hb(T.feat[:, 0:GH]), 256 * GH)
+    dma(a("l0"), hb(T.lane0[:]), 8192)
+    dma(a("X", GH, V), hb(T.feat[:, GH:V]), 256 * (V - GH))
+    dma(a("B", 0, 768), hb(T.hits[:, 0:768]), 512 * 768)
+    for lo, hi in ((768, GH), (GH, 2048), (2048, V)):
+        dma(a("B", lo, hi), (T.hits[:, lo:hi], [("X", GH, V)] if lo == 768 else []), 512 * (hi - lo))
+    dma(a("thi", p=(0, 1)), hb(T.th[:]), 32)
+
+
+    iota(a("pI", 0, 1), [[0, 1]], 0, 1, False)
+    iota(a("JI"), [[1, 256]], 0, 0, False)
+    iota(a("J2"), [[0, 16], [1, 16]], 0, 0, False)
+    iota(a("IO", p=(0, 32)), [[1, 8], [0, 64]], 0, 0)
+    iota(a("IO", p=(32, 64)), [[0, 8], [1, 64]], 0, 0)
+    send(a("X", V, WN), a("X", 0, GH))
+    iota(a("J3"), [[1, 32], [0, 16]], 0, 0, False)
+    iota(a("g24"), [[0, 3], [1, 8]], 0, 0)
+    iota(a("I384"), [[16, 3], [0, 8], [1, 16]], 1, 0)
+    for x in range(0, WD, 552):
+        iota(a("Ft", x, x + 552), [[1, 552]], x - 1280, 0)
+        if x == 1656:
+            send(a("B", V, WN), a("B", 0, GH), [("B", GH, V)])
+    for o in ops:
+        if "G" in o[0]:
+            o[2].append(("~", 0, 1))
+
+    def c(n):
+        return a("col", n, n + 1)
+    ts(a("pI", 1, 2), a("pI", 0, 1), 15, O.bitwise_and)
+    ts(a("pI", 2, 3), a("pI", 0, 1), 31, O.bitwise_and)
+    ts(a("pI", 3, 4), a("pI", 0, 1), 4, O.logical_shift_right)
+    cp(a("col", 0, 4), a("pI", 0, 4))
+    ts(a("col", 4, 7), a("JI", 0, 3), c(1), O.is_equal)
+    ts(c(7), c(1), 2.0, O.is_lt)
+    ts(c(8), c(4), 1224.0, O.mult, -124.0, O.add)
+    ts(c(9), c(5), -1280.0, O.mult, c(8), O.add)
+    aff(c(10), c(9), -1.0)
+    aff(c(11), c(9), -1.0, -127.0)
+    aff(c(12), c(4), -0.625)
+    ts(c(13), c(0), 16.0, O.add, c(4), O.mult)
+    ts(c(14), c(4), 2016.0 / 4096, O.mult, c(9), O.add)
+    ts(c(15), c(5), 32.0 / 4096, O.mult, c(14), O.add)
+    ts(c(16), c(4), -0.125, O.mult)
+    ts(a("col", 24, 32), a("JI", 0, 8), c(16), O.mult, c(15), O.add)
+    ts(a("Ib"), a("JI", 0, 128), c(0), O.is_equal)
+    ts(a("mR", 0, 256), a("J2"), c(1), O.is_equal)
+    aff(a("mR", 256, 512), a("mR", 0, 256))
+    ts(c(17), c(0), 0.0, O.is_equal, -1.0 / 64, O.mult)
+    ts(c(18), c(0), 32.0, O.is_equal, -1.0 / 4096, O.mult)
+    ts(c(19), c(0), 32.0, O.is_equal)
+    tt(c(20), c(17), c(18), O.add)
+    ts(a("WI"), a("J2", 0, 128), c(19), O.is_equal, c(20), O.mult)
+    ts(a("rst"), a("J2", 0, 256), 0.0, O.is_equal, BIG, O.mult)
+    ts(a("tc", 0, 128), a("J2", 0, 128), 0.0, O.is_equal, 1224.0, O.mult)
+    ts(a("tc", 128, 256), a("J2", 0, 128), 1.0, O.is_equal, -1280.0, O.mult)
+    tt(a("tc", 256, 384), a("tc", 0, 128), a("tc", 128, 256), O.add)
+    ts(a("offh"), a("tc", 256, 384), 3.0, O.add)
+    ts(a("ph"), a("J3", 0, 128), c(3), O.is_equal)
+    ts(a("Ih"), a("JI", 0, 128), c(0), O.is_equal)
+    ts(a("onh"), a("JI", 0, 128), 0.0, O.is_ge)
+    ts(a("j5"), a("JI", 0, 256), 1.0 / 512, O.mult)
+    cp(a("ru"), a("JI", 0, 64))
+    ts(a("blk"), a("JI", 0, 8), c(3), O.is_equal)
+    ts(a("s0"), a("blk"), c(4), O.mult)
+    ts(a("LNc"), a("JI", 0, 16), 16.0, O.mult, c(1), O.add)
+    aff(a("lnf"), a("LNc"), 1.0 / 512)
+    ts(a("Rep"), a("J3"), c(2), O.is_equal)
+    ts(a("pb"), a("J3", 0, 128), c(3), O.is_equal)
+    aff(a("nb"), a("pb"), -1.0)
+    ts(a("nsr"), a("pb"), c(7), O.mult, -1.0, O.mult)
+    aff(a("I32m"), a("Ib"))
+    ts(a("b2"), a("blk"), 2.0, O.mult)
+    ts(a("nb2"), a("blk"), -2.0, O.mult)
+    aff(a("W16c", 0, 8), a("blk"), -1.0)
+    aff(a("W16o", 0, 8), a("blk"), -1.0)
+    aff(a("W16c", 8, 16), a("blk"), c(7))
+    aff(a("W16o", 8, 16), a("W16c", 8, 16), 2.0)
+    aff(a("ns8"), a("W16c", 8, 16), -1.0)
+    ms(a("P", WN, WD), 0.0)
+    aff(c(21), c(4), 5000.0)
+    aff(a("P", MARK, MARK + 1), c(6), -30000.0, c(21))
+    ms(a("X", WN, WD), 0.0)
+    ms(a("L", WN, WD), 0.0)
+    ms(a("B", WN, WD), 0)
+    ms(a("bz"), 0.0)
+    aff(a("nIb"), a("Ib"), -1.0)
+    aff(a("hIb"), a("Ib"), 0.5)
+    ts(a("I8"), a("Ib"), 8192.0, O.mult)
+    aff(a("blkB"), a("blk"), -BIG)
+    ts(a("Big"), a("JI", 1, 145), c(13), O.is_equal)
+    ts(a("Tri"), a("JI", 0, 128), c(0), O.is_ge)
+    aff(a("onb"), a("Ib"), 0.0, 1.0)
+    aff(a("on32"), a("Ib"), 0.0, 1.0)
+    aff(a("dum", 0, 16), a("LNc"), 1.0, float(ODUM))
+    aff(a("dum", 16, 32), a("LNc"), 1.0, float(ODUM))
+    aff(a("ds", 0, 3), a("LNc", 0, 3), 1.0, 16.0)
+    aff(a("ds", 3, 6), a("LNc", 0, 3), 1.0, 16.0)
+    ts(a("lnh", 0, 1), c(0), 1.0, O.mult)
+    ts(a("lnh", 1, 2), c(0), 128.0, O.add)
+    cp(a("ou"), a("g24"))
+    ts(a("Gm", 0, 24), a("g24"), c(3), O.is_equal)
+    aff(a("Gm", 24, 48), a("Gm", 0, 24))
+    ts(a("rs8", 0, 24), a("g24"), 0.0, O.is_gt)
+    aff(a("rs8", 24, 48), a("rs8", 0, 24))
+
+    def half(n, h):
+        return a(n, 128 * h, 128 * h + 128)
+
+    def lanes(n, h, k):
+        return a(n, 2048 * h + k, 2048 * h + 2048, 16)
+
+    def places(t, lm):
+        e = str(t % 2)
+        ts(a("vu" + e), lm, 1280.0, O.add)
+        aff(a("bia" + e, 0, 16), lm, -1.0, 1.0 / 1024)
+        aff(a("vb" + e, 0, 16), lm, 1.0, 1280.0)
+        tt(a("bia" + e, 16, 32), a("bia" + e, 0, 16), a("lnf"), O.subtract)
+        grp([(a("W", 0, 256), a("Ih"), a("p16" + e)), (a("W", 0, 256), a("onh", p=(0, 1)), a("j5", p=(0, 1)))])
+        grp([(a("M1", 128 + 8 * h, 136 + 8 * h), half("p16" + e, h), a("s0")) for h in range(2)])
+        aff(a("vT" + e, 0, 16), a("M1", 128, 144), 1.0, 1280.0)
+        aff(a("vT" + e, 16, 32), a("M1", 128, 144), 1.0, 1280.0)
+        at = 0
+        for q in range(16):
+            for s in range(2):
+                act(a("junk", at, at + 16 * q + 16), a("W", 0, 16 * q + 16), F.Sign, a("bia" + e, 16 * s + q, 16 * s + q + 1), 1.0,
+                    a("acc" + e, 16 * s + q, 16 * s + q + 1))
+                at += 16 * q + 16
+
+    def conv(y, out, src, n, extra):
+        tt(a(y, 0, 256 * n), ind(src, a("ru", 0, 16 * n)), a("mR", 0, 256 * n), O.mult)
+        it = []
+        for j, o in out:
+            it += [((a(o[0], o[1] + 8 * h, o[1] + 8 * h + 8)), a(y, 256 * j + 128 * h, 256 * j + 128 * h + 128), o[2]) for h in range(2)]
+        grp(it + extra)
+
+    def rowlist(bank, lo, src, extra=()):
+        grp(list(extra) + [(a(bank, lo, lo + 16), a("Big", 15 - r, 143 - r), a(src, r, 256, 16)) for r in range(16)])
+
+    def m(n):
+        return a("tmp", 16 * n, 16 * n + 16)
+
+    def awake(t):
+        e = str(t % 2)
+        tt(m(20), a("acc" + e, 0, 16), a("acc" + e, 16, 32), O.subtract)
+        early(TM["xa"] if t else 0.0)
+        aff(a("sl" + e), m(20), 4096.0)
+        tt(m(22), a("sl" + e), a("vb" + e, 0, 16), O.add)
+        tt(m(23), m(22), a("dum", 0, 16), O.min)
+        cp(a("sv" + e), m(23))
+        act(a("aw" + e), m(20), F.Relu, 1.0, -1.0)
+
+    ts(a("l0f"), a("l0"), -1280.0, O.add)
+    tt(a("Y0"), ind(a("l0f"), a("ru", 0, 16)), a("mR", 0, 256), O.mult)
+    grp([(a("M2", 0, 256), a("ph"), a("Y0"))])
+    cp(a("p160"), a("M2", 0, 256))
+    places(0, a("l0f"))
+    for ch in range(8):
+        r = a("R%d" % (ch % 2))
+        grp([(r, a("Ib"), a("X", 512 * ch, 512 * ch + 512)), (r, a("WI", p=(0, 64)), a("IO", p=(0, 64)))])
+        aff(a("P", 512 * ch, 512 * ch + 512), r, 1.0, c(24 + ch))
+    ts(a("thf", p=(0, 1)), a("thi", p=(0, 1)), -7.5, O.add)
+    for lo, hi in ((0, 384), (384, 768), (768, 1152), (1152, GH), (GH, 2048), (2048, V)):
+        cp(a("L", lo, hi), a("B", lo, hi))
+    for x in range(V, WN, 512):
+        ts(a("L", x, x + 512), a("B", x, x + 512), float(V), O.add, float(MARK), O.min)
+
+    def rep(src, ch):
+        h, cc = divmod(ch, 4)
+        grp([(a("R%d" % (ch % 2)), a(src, 128 * h, 128 * h + 128, p=(32 * cc, 32 * cc + 32)), a("Rep", p=(32 * cc, 32 * cc + 32)))])
+
+    def big(o, i, ch):
+        tt(a(o, 512 * ch, 512 * ch + 512), a(i, 512 * ch, 512 * ch + 512), a("R%d" % (ch % 2)), O.max)
+
+    def gat(o, off, ch, more=(), lam=None):
+        aff(a(o, 512 * ch, 512 * ch + 512), ind(a("P"), a(off, 32 * ch, 32 * ch + 32)), 1.0, 0.0, more, lam)
+
+    def start(t):
+        e = str(t % 2)
+        aff(a("xm" + e), ind(a("X"), a("vu" + e)), 1.0, -127.0)
+        aff(a("Pv" + e), ind(a("P"), a("vu" + e)))
+        it = []
+        for h in range(2):
+            it += [(half("M2", h), half("xm" + e, h), a("Ib")), (half("M2", h), a("onh", p=(0, 1)), a("offh", p=(0, 1)))]
+        grp(it)
+        cp(a("xT"), a("M2", 0, 256))
+        early(TM["xt"] if t else 0.0)
+
+    start(0)
+    grp([(a("M2", 336 + 8 * h, 344 + 8 * h), a("on32", p=(0, 1)), a("thf", p=(0, 1))) for h in range(2)])
+    aff(a("tw", 0, 16), a("M2", 336, 352), -SC, 8192.0)
+    aff(a("tw", 16, 32), a("M2", 336, 352), SC)
+    awake(0)
+    for t in range(RO):
+        last = t == RO - 1
+        K, e = "K%d" % t, str(t % 2)
+        xm, Pv, vT, vb, aw = "xm" + e, "Pv" + e, a("vT" + e, 0, 16), "vb" + e, a("aw" + e)
+        cp(a("hc"), ind(a("B" if t == 0 else "L", 0, V), a("vu" + e)))
+        if t > 0:
+            u = t - 1
+            ts(a("LS%d" % u), ind(a("NL"), a("cu%d" % u, 0, 3)), float(V), O.add, float(MARK), O.min)
+            send(a("LM%d" % u), a("LS%d" % u))
+            sca(a("L", V, WD), a("K%d" % u, 16, 19), a("LM%d" % u)) if False else sca(a("L"), a("K%d" % u, 16, 19), a("LM%d" % u))
+        for h in range(2):
+            kb = "KC" if h == 0 else TM["k1"]
+            mm(k3(kb, 0, 128 * h, 128 * h + 128), half(xm, h), a("nb"), True, False)
+            mm(k3(kb, 1, 128 * h, 128 * h + 128), half(Pv, h), a("nsr"), False, False)
+            for ch in range(4 * h, 4 * h + 4):
+                gat("Pc", "hc", ch, [("acc" + e, 0, 32)] if t > 0 and ch >= TM["sg"] else [], TM["lamc"])
+                rep("xT", ch)
+                early(TM["xr"])
+                big("Mc", "Pc", ch)
+            for k in range(16):
+                mm(k3(kb, None, 128 * h + k, 128 * h + 128, 16), lanes("Pc", h, k), a("W16c"), False, False)
+            for k in range(16):
+                mm(k3(kb, 0, 128 * h + k, 128 * h + 128, 16), lanes("Mc", h, k), a("b2"), False, k == 15)
+            y, key = k3(kb, 1, 128 * h, 128 * h + 128), k3(kb, 0, 128 * h, 128 * h + 128)
+            act(half("aV", h), (y[0], y[1] + key[1]) + y[2:], F.Abs)
+            act(half("mv", h), half("aV", h), F.Relu, 4090.0, -SC)
+            tt(half("A", h), key, half("mv", h), O.add)
+            scan(half("sc", h), half("rst", h), half("A", h), 0.0, O.add, O.min)
+        act(a("mw"), a("aV"), F.Relu, 8192.0, -2 * SC)
+        kmin = a("sc", 15, 256, 16)
+        for h in range(2):
+            lo, hi = 8 * h, 8 * h + 8
+            ts(a("kb", lo, hi), a("sc", 128 * h + 15, 128 * h + 128, 16), 4096.0, O.mult, 2048.0, O.add)
+            ts(a("bI", lo, hi), a("kb", lo, hi), 4095, O.bitwise_and)
+            tt(half("Yb", h), ind(a("bI", lo, hi), a("ru", 0, 8)), a("mR", 0, 128), O.mult)
+            grp([(a("M1", lo, hi), half("Yb", h), a("blk"))])
+            cp(a("bu", lo, hi), a("M1", lo, hi))
+            aff(half("xb", h), ind(a("X"), a("bu", lo, hi)), 1.0, -127.5)
+            cp(half("ho", h), ind(a("L", 0, WN), a("bu", lo, hi)))
+            early(TM["xh"] if h == 0 else 0.0)
+            z = a("M2", 256 + 128 * h, 384 + 128 * h)
+            grp([(z, half(xm, h), a("hIb")), (z, a("onh", p=(0, 1)), a("offh", p=(0, 1))), (z, half("xb", h), a("hIb"))])
+            ts(half("zT", h), z, MAGIC, O.add, MAGIC, O.subtract)
+            early(TM["xh"] if h == 0 else 0.0)
+        bT = a("bz", 0, 256, 16)
+        cp(bT, a("bI", 0, 16))
+        aff(a(vb, 16, 32), a("M1", 0, 16))
+        grp([(half("M2", h), half("bz", h), a("I32m")) for h in range(2)])
+        aff(a("bR"), a("M2", 0, 256))
+        sca(a("B"), a("sv" + e), a("bR"))
+        ts(a("B16"), ind(a("B", 0, WN), a("bu")), -2048.0, O.add)
+        rowlist("M1", 16, "B16", [(a("M1", 16, 32), a("I32m"), a("sl" + e))])
+        ts(a("xu"), a("M1", 16, 32), 2048.0, O.add, float(MARK), O.min)
+        aff(a("Px"), ind(a("P"), a("xu")))
+        aff(a("Pb"), ind(a("P"), a("bu")))
+        for h in range(2):
+            z = a("W", 256 + 128 * h, 384 + 128 * h)
+            grp([(z, half("zT", h), a("Ih"))])
+            aff(half("zm", h), z, 1.0, c(11))
+        aff(a("zr"), a("W", 256, 512), 1.0, c(10))
+        it = []
+        for h in range(2):
+            it += [(a("M1", 48 + 8 * h, 56 + 8 * h), half("Pb", h), a("W16c", 8, 16)), (a("M1", 48 + 8 * h, 56 + 8 * h), half(Pv, h), a("ns8"))]
+        for h in range(2):
+            it += [(a("M1", 32 + 8 * h, 40 + 8 * h), half(Pv, h), a("ns8")), (a("M1", 32 + 8 * h, 40 + 8 * h), half("Px", h), a("W16c", 8, 16))]
+        grp(it)
+        n2 = 16 if last else 32
+        if not last:
+            ts(a("kc"), a("A", t, 256, 16), 4096.0, O.mult, 2048.0, O.add)
+            ts(a("bI", 16, 32), a("kc"), 4095, O.bitwise_and)
+        tt(a("tmp", 0, n2), a("bI", 0, n2), a("vT" + e, 0, n2), O.subtract)
+        ts(a("tmp", 32, 32 + n2), a("bI", 0, n2), float(V), O.is_lt)
+        tt(a("tmp", 64, 64 + n2), a("tmp", 0, n2), a("tmp", 32, 32 + n2), O.mult)
+        add({"V": vts(m(13), m(4), 0.0, O.is_le, BIG, O.mult), "S": sact(m(13), m(4), F.Relu, BIG, -BIG)}, m(4)[1], m(13)[1])
+        tt(m(14), bT, m(4), O.subtract)
+        aff(a("tv", 48, 64), m(14), 1.0 / 4096, 4081.5)
+        join = a("tj", 0, 16)
+        tt(join, a("M1", 32, 48), m(13), O.is_equal)
+        act(a("tw", 48, 64), a("M1", 48, 64), F.Abs)
+        aff(a("tw", 32, 48), kmin, SC, 8192.0)
+        if not last:
+            aff(m(15), m(2), -1.0, 1.0)
+            tt(m(16), m(15), m(5), O.mult)
+            tt(m(17), m(16), m(4), O.add)
+            aff(m(7), join, -1.0, 1.0)
+            tt(a("tj", 16, 32), m(7), m(17), O.mult)
+            conv("Yc", [(0, ("M1", 64, a("blkB"))), (0, ("M1", 80, a("blkB"))), (1, ("M1", 96, a("blk")))], a("tj"), 2,
+                 [(a("M1", 64, 96), a("I32m"), a("dum"))])
+        else:
+            conv("Yc", [(0, ("M1", 64, a("blkB"))), (0, ("M1", 80, a("blkB")))], join, 1, [(a("M1", 64, 96), a("I32m"), a("dum"))])
+        for x in range(4):
+            aff(a("tq", 16 * x, 16 * x + 16), join, (-2 if x < 2 else 2) * BIG * SC, (1 if x < 2 else -1) * BIG * SC)
+        tt(a("tz"), a("tq"), a("tw"), O.min)
+        tt(a("tv", 0, 16), a("tz", 0, 16), a("tz", 32, 48), O.max)
+        aff(a("tv", 16, 32), join, -2 * SC, SC)
+        act(a("rp"), ind(a("tv", 48, 64), a("ru", 0, 16)))
+        tt(a("tmp", 176, 208), a("M1", 64, 96), a(vb), O.max)
+        cp(a(K, 20, 36), a("tmp", 192, 208))
+        cp(a(K, 0, 16), a("tmp", 176, 192))
+        sca(a("Ft"), a(K, 20, 36), a("p16" + e))
+        if not last:
+            tt(m(6), a("M1", 96, 112), aw, O.mult)
+            tt(m(8), m(6), a(vb, 0, 16), O.add)
+            cp(a("tu"), m(8))
+            cp(a("p16" + str((t + 1) % 2)), ind(a("Ft", 0, V), a("tu")))
+            rowlist("M1", 112, "p16" + str((t + 1) % 2))
+            act(m(10), vT, F.Relu, 1.0 - GH)
+            tt(a("tl"), join, m(10), O.is_gt)
+            ts(a("vq"), vT, float(GH), O.subtract, 0.0, O.min)
+            ts(a("bq"), bT, float(GH), O.subtract, 0.0, O.min)
+            grp([(a("M2", 0, 16), a("Tri"), a("tl")), (a("M2", 8, 16), a("onb"), a("tl", 0, 8))])
+            grp([(a("W", 256, 512), a("I32m"), a(Pv)), (a("W", 256, 512), a("nIb"), a(xm)), (a("W", 256, 512), a("Ib"), a("zm"))])
+            aff(a("PZ%d" % t, 0, 256), a("W", 256, 512))
+            tt(a("s1"), a("M2", 0, 16), a("tl"), O.mult)
+            for h in range(2):
+                tt(a("OH", 384 * h, 384 * h + 384), ind(a("s1", 8 * h, 8 * h + 8), a("ou")), a("I384"), O.is_equal)
+            it = []
+            for q in range(3):
+                for h in range(2):
+                    oh = a("OH", 384 * h + 128 * q, 384 * h + 128 * q + 128)
+                    it += [(a("M2", 16 + 8 * q, 24 + 8 * q), oh, a("vq", 8 * h, 8 * h + 8)), (a("M2", 40 + 8 * q, 48 + 8 * q), oh, a("bq", 8 * h, 8 * h + 8)),
+                           (a("M2", 64 + q, 65 + q), oh, a("lnh", h, h + 1))]
+            grp(it)
+            cp(a("cu%d" % t, 0, 3), a("M2", 64, 67))
+            tt(a("gs"), a("M2", 16, 64), a("Gm"), O.mult)
+            scan(a("gs2"), a("rs8"), a("gs"), 0.0, O.mult, O.add)
+            sums = a("gs2", 7, 48, 8)
+            ts(a("gs3", 0, 6), sums, 0.0, O.is_ge)
+            tt(a("gs4", 0, 6), a("gs3", 0, 6), a("ds", 0, 6), O.mult)
+            tt(a("EM%d" % t, 48, 54), a("gs4", 0, 6), sums, O.add)
+            aff(a("EM%d" % t, 0, 48), ind(a("PZ%d" % t, 0, 256), a("cu%d" % t, 0, 3)), 1.0, c(12))
+            send(a("PZ%d" % t, 256, 310), a("EM%d" % t, 0, 54))
+            places(t + 1, a("M1", 112, 128))
+            awake(t + 1)
+        else:
+            for u in (2, 1, 0):
+                aff(a("DT%d" % u, 0, 256), ind(a("Ft"), a("K%d" % u, 0, 16)))
+                sca(a("Ft"), a("K%d" % u, 20, 36), a("DT%d" % u, 0, 256))
+        sca(a("X"), a(K, 0, 16), a("zr"))
+        if last:
+            dma(hb(T.yx[:]), a("X", 0, V), 256 * V)
+        mm(a("KZ", 0, 256), a("I32m"), a("A"), True, False)
+        for h in range(2):
+            for k in range(16):
+                mm(a("KZ", 128 * h + k, 128 * h + 128, 16), lanes("Mc", h, k), a("nb2"), False, False)
+        for h in range(2):
+            mm(half("KZ", h), half(xm, h), a("pb"), False, False)
+            mm(half("KZ", h), half("zm", h), a("nb"), False, False)
+        mm(a("KZ", 0, 256), a("Ib"), a("mw"), False, False)
+        for ch in range(8):
+            gat("Po", "ho", ch)
+        for x in range(16):
+            act(a("gt", 16 * x, 16 * x + 16), a("A", 16 * x, 16 * x + 16), F.Relu, a("tv", x, x + 1), a("tv", 16 + x, 17 + x))
+            act(a("lt", 16 * x, 16 * x + 16), a("A", 16 * x, 16 * x + 16), F.Relu, a("tz", 16 + x, 17 + x), -SC)
+        for h in range(2):
+            y, key = k3("KO", 1, 128 * h, 128 * h + 128), k3("KO", 0, 128 * h, 128 * h + 128)
+            mm(y, half(Pv, h), a("nsr"), True, False)
+            mm(y, half("Pb", h), a("nsr"), False, False)
+            mm(key, half("zm", h), a("nb"), False, False)
+            for ch in range(4 * h, 4 * h + 4):
+                rep("zT", ch)
+                early(TM["xz"])
+                big("Mz", "Pc", ch)
+                big("Mo", "Po", ch)
+            for k in range(16):
+                mm(k3("KO", None, 128 * h + k, 128 * h + 128, 16), lanes("Po", h, k), a("W16o"), False, k == 15)
+            act(half("aY", h), y, F.Abs)
+            aff(half("Ao", h), key)
+            mm(a("KZ", 256 + 128 * h, 384 + 128 * h), a("I32m"), half("Ao", h), False, False)
+            if h == 1:
+                tt(a("xo"), ind(a("tz", 48, 64), a("ru", 0, 16)), a("aY"), O.is_equal)
+                mm(a("KZ", 0, 256), a("Ib"), a("gt"), False, False)
+                mm(a("KZ", 256, 512), a("Ib"), a("lt"), False, False)
+                mm(a("KZ", 256, 512), a("I8"), a("xo"), False, False)
+            for k in range(16):
+                mm(a("KZ", 128 * h + k, 128 * h + 128, 16), lanes("Mz", h, k), a("b2"), False, False)
+            for k in range(16):
+                mm(a("KZ", 256 + 128 * h + k, 384 + 128 * h, 16), lanes("Mo", h, k), a("b2"), False, h == 1 and k == 15)
+        kz = a("KZ", 0, 256)
+        tt(a("t1"), (kz[0], [("KZ", 0, 512)]) + kz[2:], a("rp"), O.min)
+        tt(a("t2"), a("KZ", 256, 512), a("t1"), O.min)
+        grp([(half("M2", h), half("t2", h), a("I32m")) for h in range(2)])
+        ts(a("ki"), a("M2", 0, 256), 4096.0, O.mult, 2048.0, O.add)
+        ts(a("NL"), a("ki"), 4095, O.bitwise_and)
+        sca(a("L"), a("sv" + e), a("NL"))
+        if not last:
+            pz = "PZ%d" % t
+            ts(a(K, 16, 19), a(pz, 304, 307), float(WN), O.add)
+            ts(a(K, 36, 39), a(pz, 307, 310), float(WN), O.add)
+            sca(a("P"), a(K, 0, 19), a(pz, 0, 304))
+            sca(a("P"), a(K, 20, 39), a(pz, 0, 304))
+            for u in range(t - 1, -1, -1):
+                aff(a("DT%d" % u), ind(a("P"), a("K%d" % u, 0, 19)))
+                sca(a("P"), a("K%d" % u, 20, 39), a("DT%d" % u))
+            start(t + 1)
+    dma(hb(T.yl[:]), a("L", 0, V), 512 * V)
+    for x in range(0, V, 1280):
+        aff(a("YF", x, x + 1280), a("Ft", x, x + 1280), 1.0, 1280.0, (), 0.0)
+    for gg in range(8):
+        dma(hb(T.yf[gg:gg + 1, :]), a("YF", p=(16 * gg, 16 * gg + 1)), 4 * V)
+
+    emit(g, T, ops)
+
+
+def _deps(ops, eng):
+    acc, deps, lastg, lasty = {}, [], [], []
+    for n, (alts, rd, wr, kind, sem, cnt, _x) in enumerate(ops):
+        d = set()
+        pe = "P" in alts
+        use = [(r, False) for r in rd] + [(r, True) for r in wr if eng is None or r[0] != "~"]
+        for (name, lo, hi), w in use:
+            ps = name in PSUM
+            for (m, w2, lo2, hi2) in acc.get(name, []):
+                if pe and ps and "P" in ops[m][0]:
+                    if eng is None:
+                        d.add(m)
+                elif (lo < hi2 and lo2 < hi and (w or w2)) or (ps and eng is not None and eng[m] != eng[n]):
+                    d.add(m)
+        if eng is not None and eng[n] == "G" and kind == "c":
+            d.update(lastg)
+            lastg[:] = [n]
+        if eng is None and kind == "a":
+            d.add(n - 1)
+        if eng is None and kind == "d":
+            d.update(lasty)
+            lasty[:] = [n]
+        for (name, lo, hi), w in use:
+            lst = acc.setdefault(name, [])
+            if w and name not in PSUM:
+                lst[:] = [x for x in lst if not (lo <= x[2] and x[3] <= hi)]
+            elif name in PSUM and len(lst) > 200:
+                del lst[:50]
+            lst.append((n, w, lo, hi))
+        deps.append(d)
+    return deps
+
+
+def _order(ops):
+    deps = _deps(ops, None)
+    n = len(ops)
+    wake = TM["wake"]
+
+    def least(i):
+        o = ops[i]
+        if o[3] == "a":
+            return 0.0
+        x = min(v[1] for v in o[0].values())
+        return x if o[3] == "c" else TM["dfix"] + x / TM["bw"] if o[2] or o[3] == "r" or i >= n - 11 else 100.0
+    succ = [[] for _ in range(n)]
+    for i in range(n):
+        for m in deps[i]:
+            succ[m].append(i)
+    pri = [0.0] * n
+    for i in range(n - 1, -1, -1):
+        pri[i] = least(i) + ops[i][6][0] + max([pri[j] + (0.0 if "P" in ops[i][0] and "P" in ops[j][0] else wake) for j in succ[i]] + [0.0])
+    banks = [set(r[0] for r in o[1] + o[2] if r[0] in PSUM) for o in ops]
+    best = None
+    rnd = np.random.RandomState(TM["seed"])
+    for it in range(TM["it"]):
+        order, eng, fin = _greedy(ops, deps, succ, pri)
+        LOG.append(max(fin))
+        if best is None or max(fin) < best[0]:
+            best = (max(fin), order, eng, fin)
+        back = _pass(ops, succ, deps, banks, best[3], best[2])[1]
+        noise = rnd.normal(0.0, TM["noise"] * min(it, 1), n)
+        pri = [TM["mix"] * back[i] + (1.0 - TM["mix"]) * (best[0] - best[3][i]) + float(noise[i]) for i in range(n)]
+    return best[1], best[2]
+
+
+def _greedy(ops, deps, succ, pri):
+    n, wake = len(ops), TM["wake"]
+    fin = [0.0] * n
+    left = [len(d) for d in deps]
+    rdy = [0.0] * n
+    ready = [i for i in range(n) if left[i] == 0]
+    free = {q: 0.0 for q in "VSPGY"}
+    bank = {b: ("", 0.0) for b in PSUM}
+    banks = [set(r[0] for r in o[1] + o[2] if r[0] in PSUM) for o in ops]
+    pipe = [0.0]
+    start, eng = [0.0] * n, [None] * n
+    order = []
+    while ready:
+        cand = []
+        for i in ready:
+            best = None
+            if not ops[i][0]:
+                best = (rdy[i], rdy[i], None)
+            for q in ops[i][0]:
+                s = max(free[q], rdy[i])
+                for b in banks[i]:
+                    if bank[b][0] != q:
+                        s = max(s, bank[b][1] + wake)
+                lam = ops[i][0][q][2] if len(ops[i][0][q]) > 2 and ops[i][0][q][2] is not None else TM["lam"]
+                key = s + ops[i][0][q][1] * ((1.0 + lam) if q == "V" else 1.0)
+                if best is None or key < best[0]:
+                    best = (key, s, q)
+            cand.append((best[1], i, best[2]))
+        lo = min(x[0] for x in cand)
+        s, i, q = max((x for x in cand if x[0] <= lo + TM["look"]), key=lambda x: (pri[x[1]], -x[1]))
+        ready.remove(i)
+        order.append(i)
+        start[i], eng[i] = s, q
+        if ops[i][3] == "c":
+            end = s + ops[i][0][q][1]
+            free[q] = end
+            for b in banks[i]:
+                bank[b] = (q, end)
+        elif ops[i][3] == "a":
+            end = s
+        else:
+            free[q] = s + 100.0
+            pipe[0] = max(pipe[0], s + TM["dfix"]) + ops[i][0][q][1] / TM["bw"]
+            end = pipe[0]
+        fin[i] = end
+        for j in succ[i]:
+            after = s if (ops[i][3] == "d" and ops[j][3] == "d" and not (ops[j][1] and ops[i][2])) or (q == "P" and "P" in ops[j][0]) or (
+                ops[i][3] == "r" and "G" in ops[j][0]) else end + wake
+            rdy[j] = max(rdy[j], after)
+            left[j] -= 1
+            if left[j] == 0:
+                ready.append(j)
+    return order, eng, fin
+
+
+def _gap(busy, t, c, pad):
+    lo, hi = 0, len(busy)
+    while lo < hi:
+        mid = (lo + hi) // 2
+        if busy[mid][1] + pad <= t:
+            lo = mid + 1
+        else:
+            hi = mid
+    while lo < len(busy) and busy[lo][0] < t + c + pad:
+        t = max(t, busy[lo][1] + pad)
+        lo += 1
+    return t
+
+
+def _put(busy, s, e):
+    lo, hi = 0, len(busy)
+    while lo < hi:
+        mid = (lo + hi) // 2
+        if busy[mid][0] < s:
+            lo = mid + 1
+        else:
+            hi = mid
+    busy.insert(lo, (s, e))
+
+
+def _pass(ops, pred, succ, banks, pri, fixed):
+    n, wake = len(ops), TM["wake"]
+    left = [len(d) for d in pred]
+    ready = [i for i in range(n) if left[i] == 0]
+    busy = {q: [] for q in "VSPGYD"}
+    bank = {b: {q: [] for q in "VSP"} for b in PSUM}
+    start, end, eng = [0.0] * n, [0.0] * n, [None] * n
+    while ready:
+        i = max(ready, key=lambda x: pri[x])
+        ready.remove(i)
+        alts, kind = ops[i][0], ops[i][3]
+        r = 0.0
+        for m in pred[i]:
+            if kind == "d" and ops[m][3] == "d" and not (ops[max(i, m)][1] and ops[min(i, m)][2]):
+                x = start[m]
+            elif "G" in alts and "G" in ops[m][0] and ops[min(i, m)][3] == "r":
+                x = start[m]
+            elif "P" in alts and "P" in ops[m][0]:
+                x = end[m]
+            else:
+                x = end[m] + wake
+            if x > r:
+                r = x
+        best = (r, r, None, r)
+        for z, q in enumerate([fixed[i]] if fixed and alts else alts):
+            c = alts[q][1] if kind == "c" else 100.0
+            s = r
+            while True:
+                s0 = s
+                s = _gap(busy[q], s, c, 0.0)
+                for b in banks[i]:
+                    for o in "VSP":
+                        if o != q:
+                            s = _gap(bank[b][o], s, c, wake)
+                if s == s0:
+                    break
+            lam = alts[q][2] if len(alts[q]) > 2 and alts[q][2] is not None else TM["lam"]
+            key = s + c * ((1.0 + lam) if q == "V" else 1.0)
+            if z == 0 or key < best[0]:
+                best = (key, s, q, s + c)
+        s, q, e = best[1:]
+        if q is not None:
+            _put(busy[q], s, e)
+            for b in banks[i]:
+                _put(bank[b][q], s, e)
+            if kind != "c":
+                c = alts[q][1] / TM["bw"]
+                d = s + TM["dfix"] if fixed else _gap(busy["D"], s + TM["dfix"], c, 0.0)
+                _put(busy["D"], d, d + c)
+                e = d + c
+        start[i], end[i], eng[i] = s, e, q
+        for j in succ[i]:
+            left[j] -= 1
+            if left[j] == 0:
+                ready.append(j)
+    return start, end, eng
+
+
+def _order2(ops):
+    n = len(ops)
+    pred = [sorted(d) for d in _deps(ops, None)]
+    succ = [[] for _ in range(n)]
+    for i in range(n):
+        for m in pred[i]:
+            succ[m].append(i)
+    banks = [set(r[0] for r in o[1] + o[2] if r[0] in PSUM) for o in ops]
+    pri = [0.0] * n
+    for i in range(n - 1, -1, -1):
+        o = ops[i]
+        x = min([v[1] for v in o[0].values()] + [1e9]) if o[0] else 0.0
+        x = x if o[3] in "ca" else TM["dfix"] + x / TM["bw"]
+        pri[i] = x + o[6][0] + max([pri[j] + TM["wake"] for j in succ[i]] + [0.0])
+    best = None
+    for it in range(TM["it"]):
+        start, end, eng = _pass(ops, pred, succ, banks, pri, None)
+        if best is None or max(end) < best[0]:
+            best = (max(end), start, eng)
+        LOG.append(max(end))
+        bs, be, _ = _pass(ops, succ, pred, banks, end, eng)
+        pri = be
+    return sorted(range(n), key=lambda i: (best[1][i], i)), best[2]
+
+
+LOG = []
+PLAN = []
+
+
+def emit(g, T, ops):
+    qs = {"V": g.vector, "S": g.scalar, "P": g.tensor, "G": g, "Y": g.sync}
+    if not PLAN:
+        order, eng = _order(ops)
+        eng = [eng[i] for i in order]
+        PLAN.extend([order, eng, _deps([ops[i] for i in order], eng)])
+    order, eng, deps = PLAN
+    ops = [ops[i] for i in order]
+    strm = [eng[n] if o[3] == "c" else o[4] for n, o in enumerate(ops)]
+    known = {q: {} for q in qs}
+    after, waits = [], []
+    for n, o in enumerate(ops):
+        w, vc = [], {}
+        if eng[n] is not None:
+            kn = known[eng[n]]
+            for m in sorted(deps[n], reverse=True):
+                if kn.get(strm[m], -1) < m:
+                    w.append(m)
+                    for s in after[m]:
+                        if kn.get(s, -1) < after[m][s]:
+                            kn[s] = after[m][s]
+            vc = dict(kn)
+        vc[strm[n]] = n
+        after.append(vc)
+        waits.append(w)
+    need = set(m for w in waits for m in w)
+    count, at = {}, {}
+    for n, o in enumerate(ops):
+        if o[3] != "c":
+            at[n] = (o[4], o[5])
+        elif n in need:
+            count[eng[n]] = count.get(eng[n], 0) + 1
+            at[n] = ("e" + eng[n], count[eng[n]])
+    for n, o in enumerate(ops):
+        if eng[n] is None:
+            continue
+        for m in waits[n]:
+            qs[eng[n]].wait_ge(T.sem[at[m][0]], at[m][1])
+        ins = o[0][eng[n]][0]()
+        if o[3] == "d":
+            ins.then_inc(T.sem[o[4]], 16)
+        elif o[3] == "c" and n in need:
+            ins.then_inc(T.sem[at[n][0]], 1)
+    for n, o in enumerate(ops):
+        if o[3] != "c" and n not in need:
+            g.wait_ge(T.sem[at[n][0]], at[n][1])

@@ -26,15 +26,15 @@ def _sb(dtype, size, **kw):
     SCRATCH[pool] = ("sbuf", [128, at], dtype)
 
 
-_sb(F32, 4, P=WD, L=WD, Ft=WD, Pc=4096, Po=4096, YF=V, Pv0=256, Pv1=256, Pb=256, Px=256, A=256, Ao=256, sc=256, aY=256, bz=256, bR=256,
-    Ya=256, Yb=256, Yc=512, rp=256, aV=256, mv=256, t1=256, t2=256, tv=64, blkB=8, tj=32, vb0=32, vb1=32, tmp=512, tc=384, acc0=32, acc1=32,
+_sb(F32, 4, P=WD, L=WD, Ft=WD, Pc=4096, Po=4096, YF=V, Pv0=256, Pv1=256, Pb=256, Px=256, A=256, Ao=256, sc=256, aY=256, bR=256,
+    Ya=256, Yb=256, Yc=512, rp=256, aV=256, mv=256, t1=256, t2=256, tv=64, tj=32, vb0=32, vb1=32, tmp=512, tc=384, acc0=32, acc1=32,
     bia0=32, bia1=32, vT0=32, vT1=32, aw0=16, aw1=16, sl0=16, sl1=16, tw=64, tq=64, tz=64, s1=16, l0f=16,
-    I32m=128, nsr=128, W16c=16, W16o=16, ns8=8, blk=8, mR=512, rst=256, rs8=48, Gm=48, I384=384, col=32, LNc=16, dum=32,
+    I32m=128, nsr=128, W16c=16, W16o=16, ns8=16, blk=8, mR=512, rst=256, rs8=48, Gm=48, I384=384, col=32, LNc=16, dum=32,
     ds=8, thf=8, on32=128, lnf=16, g24=24, gs=48, gs2=48, gs3=8, gs4=8, LM0=48, LM1=48, LM2=48, DT0=304, DT1=304, DT2=304,
     PZ0=312, PZ1=312, PZ2=312, EM0=56, EM1=56, EM2=56, LS0=48, LS1=48, LS2=48)
-_sb(BF, 2, X=WD, xm0=256, xm1=256, xb=256, zr=256, zm=256, gt=256, lt=256, mw=256, junk=4352, Ib=128, nIb=128, hIb=128, pb=128, nb=128, IO=512, WI=128,
+_sb(BF, 2, X=WD, xm0=256, xm1=256, xb=256, zr=256, zm=256, gt=256, lt=256, mw=256, xw=256, Yj=256, blkB=8, junk=4352, Ib=128, nIb=128, hIb=128, I2b=128, pb=128, nb=128, IO=512, WI=128,
     Tri=128, onb=128, tl=16)
-_sb(H16, 2, Mc=4096, Mo=4096, Mz=4096, xT=256, zT=256, xo=256, p160=256, p161=256, B16=256, OH=768, Ih=128,
+_sb(H16, 2, Mc=4096, Mo=4096, Mz=4096, xT=256, zT=256, xo=256, bz=256, p160=256, p161=256, B16=256, OH=768, Ih=128,
     I8=128, Rep=512, b2=8, nb2=8, s0=8, Big=144, onh=128, offh=128, j5=256, ph=128, Y0=256, vq=16, bq=16, lnh=2)
 _sb(I32, 4, B=WD, NL=256, ki=256, kb=16, kc=16, bI=32, JI=256, J2=256, J3=512, pI=8, l0=16, thi=8)
 _sb(U16, 2, hc=256, ho=256, vu0=16, vu1=16, bu=16, sv0=16, sv1=16, xu=16, tu=16, ru=64, ou=24, cu0=4, cu1=4, cu2=4,
@@ -48,13 +48,32 @@ PSUM = ("R0", "R1", "KZ", "M1", "M2", "W", "KC", "KO")
 SEMAPHORES = ["eV", "eS", "eP", "eG"] + ["d%d" % i for i in range(24)] + ["r%d" % i for i in range(8)] + ["l%d" % i for i in range(8)]
 
 TM = dict(cy=1.04, g=1.56, s=3.8, pe=0.53, fix=60.0, wake=100.0, bw=200.0, dfix=2000.0, look=150.0, lam=4.0, lamc=0.5, sg=8, xa=20000.0,
-          xr=1000.0, xz=0.0, xt=0.0, k1="KC", xh=35000.0, it=30, seed=1, noise=40.0, mix=1.0)
+          xr=1000.0, xz=0.0, xt=0.0, k1="KC", xh=35000.0, xo=0, xp=1, mw=1, hc=0, r3=1, whole=999, span=150, more=3.0, moves=8000, heat=100.0, lamx=0.5, lamy=4.0, gv=1536, yx=0.0, it=40, seed=1, noise=30.0, looks=[60.0, 100.0, 150.0, 220.0])
+
+
+CLOCKS = [dict(cy=0.83, pe=0.42, g=1.56, s=3.8, fix=30.0, wake=50.0, bw=250.0), dict(cy=0.9, pe=0.45, g=1.2, s=2.2, fix=40.0, wake=60.0, bw=250.0),
+          dict(cy=1.04, pe=0.52, g=1.56, s=3.8, fix=40.0, wake=70.0, bw=200.0), dict(cy=1.2, pe=0.6, g=1.9, s=5.0, fix=40.0, wake=60.0, bw=250.0),
+          dict(cy=1.1, pe=0.55, g=1.6, s=4.0, fix=50.0, wake=170.0, bw=130.0)]
+for _c in CLOCKS:
+    _c["dfix"] = 3200.0 if _c["bw"] < 150 else 2000.0
 
 
 def rank_program(g, core, T, topo):
-    rank = T.rank_of(core)
-    if rank is None:
+    if T.rank_of(core) is None:
         return
+    if not PLAN:
+        every = []
+        for clock in CLOCKS:
+            TM.update(clock)
+            every.append(calls(g, core, T, topo))
+        order, eng = _order(every)
+        eng = [eng[i] for i in order]
+        PLAN.extend([order, eng, _deps([every[0][i] for i in order], eng)])
+    emit(g, T, calls(g, core, T, topo))
+
+
+def calls(g, core, T, topo):
+    rank = T.rank_of(core)
     O, F = AluOpType, ActivationFunctionType
     dst = T.cores[(rank - 1) % len(T.cores)]
     rid, pid = topo.addr(dst)[0], topo.addr(dst)[1]
@@ -184,8 +203,8 @@ def rank_program(g, core, T, topo):
     iota(a("I384"), [[16, 3], [0, 8], [1, 16]], 1, 0)
     for x in range(0, WD, 552):
         iota(a("Ft", x, x + 552), [[1, 552]], x - 1280, 0)
-        if x == 1656:
-            send(a("B", V, WN), a("B", 0, GH), [("B", GH, V)])
+    iota(a("B", V, 3488), [[0, 928]], 0, 0, False)
+    iota(a("B", 3488, WD), [[0, 928]], 0, 0, False)
     for o in ops:
         if "G" in o[0]:
             o[2].append(("~", 0, 1))
@@ -202,6 +221,7 @@ def rank_program(g, core, T, topo):
     ts(c(9), c(5), -1280.0, O.mult, c(8), O.add)
     aff(c(10), c(9), -1.0)
     aff(c(11), c(9), -1.0, -127.0)
+    aff(c(22), c(11), 1.0, -MAGIC)
     aff(c(12), c(4), -0.625)
     ts(c(13), c(0), 16.0, O.add, c(4), O.mult)
     ts(c(14), c(4), 2016.0 / 4096, O.mult, c(9), O.add)
@@ -236,19 +256,19 @@ def rank_program(g, core, T, topo):
     ts(a("nsr"), a("pb"), c(7), O.mult, -1.0, O.mult)
     aff(a("I32m"), a("Ib"))
     ts(a("b2"), a("blk"), 2.0, O.mult)
-    ts(a("nb2"), a("blk"), -2.0, O.mult)
+    aff(a("I2b"), a("Ib"), 4.0)
     aff(a("W16c", 0, 8), a("blk"), -1.0)
     aff(a("W16o", 0, 8), a("blk"), -1.0)
     aff(a("W16c", 8, 16), a("blk"), c(7))
     aff(a("W16o", 8, 16), a("W16c", 8, 16), 2.0)
-    aff(a("ns8"), a("W16c", 8, 16), -1.0)
+    aff(a("ns8", 0, 16, 2), a("W16c", 8, 16), -1.0)
+    aff(a("ns8", 1, 16, 2), a("W16c", 8, 16), -1.0)
     ms(a("P", WN, WD), 0.0)
     aff(c(21), c(4), 5000.0)
     aff(a("P", MARK, MARK + 1), c(6), -30000.0, c(21))
     ms(a("X", WN, WD), 0.0)
     ms(a("L", WN, WD), 0.0)
-    ms(a("B", WN, WD), 0)
-    ms(a("bz"), 0.0)
+    ts(a("bz"), a("JI"), 0.0, O.mult)
     aff(a("nIb"), a("Ib"), -1.0)
     aff(a("hIb"), a("Ib"), 0.5)
     ts(a("I8"), a("Ib"), 8192.0, O.mult)
@@ -297,7 +317,7 @@ def rank_program(g, core, T, topo):
         it = []
         for j, o in out:
             it += [((a(o[0], o[1] + 8 * h, o[1] + 8 * h + 8)), a(y, 256 * j + 128 * h, 256 * j + 128 * h + 128), o[2]) for h in range(2)]
-        grp(it + extra)
+        grp(extra + it)
 
     def rowlist(bank, lo, src, extra=()):
         grp(list(extra) + [(a(bank, lo, lo + 16), a("Big", 15 - r, 143 - r), a(src, r, 256, 16)) for r in range(16)])
@@ -310,8 +330,8 @@ def rank_program(g, core, T, topo):
         tt(m(20), a("acc" + e, 0, 16), a("acc" + e, 16, 32), O.subtract)
         early(TM["xa"] if t else 0.0)
         aff(a("sl" + e), m(20), 4096.0)
-        tt(m(22), a("sl" + e), a("vb" + e, 0, 16), O.add)
-        tt(m(23), m(22), a("dum", 0, 16), O.min)
+        grp([(a("M1", 144, 160), a("I32m"), a("vb" + e, 0, 16)), (a("M1", 144, 160), a("I32m"), a("sl" + e))])
+        tt(m(23), a("M1", 144, 160), a("dum", 0, 16), O.min)
         cp(a("sv" + e), m(23))
         act(a("aw" + e), m(20), F.Relu, 1.0, -1.0)
 
@@ -327,23 +347,35 @@ def rank_program(g, core, T, topo):
     ts(a("thf", p=(0, 1)), a("thi", p=(0, 1)), -7.5, O.add)
     for lo, hi in ((0, 384), (384, 768), (768, 1152), (1152, GH), (GH, 2048), (2048, V)):
         cp(a("L", lo, hi), a("B", lo, hi))
-    for x in range(V, WN, 512):
-        ts(a("L", x, x + 512), a("B", x, x + 512), float(V), O.add, float(MARK), O.min)
+    for x in range(0, GH, 384):
+        if x < TM["gv"]:
+            ts(a("Po", GH + x, GH + x + 384), a("B", x, x + 384), float(V), O.add, float(MARK), O.min)
+        else:
+            act(a("Po", x, x + 384), a("L", x, x + 384), F.Relu, float(GH), -1.0)
+            act(a("Po", GH + x, GH + x + 384), a("Po", x, x + 384), F.Identity, float(MARK), -1.0)
+    send(a("L", V, WN), a("Po", GH, 2 * GH), [("B", GH, V)])
 
     def rep(src, ch):
         h, cc = divmod(ch, 4)
-        grp([(a("R%d" % (ch % 2)), a(src, 128 * h, 128 * h + 128, p=(32 * cc, 32 * cc + 32)), a("Rep", p=(32 * cc, 32 * cc + 32)))])
+        grp([(a(rb(src, ch)), a(src, 128 * h, 128 * h + 128, p=(32 * cc, 32 * cc + 32)), a("Rep", p=(32 * cc, 32 * cc + 32)))])
+
+    def rb(src, ch):
+        return ("R0", "R1", "KZ")[ch % 3] if src == "xT" and TM["r3"] else "R%d" % (ch % 2)
 
     def big(o, i, ch):
-        tt(a(o, 512 * ch, 512 * ch + 512), a(i, 512 * ch, 512 * ch + 512), a("R%d" % (ch % 2)), O.max)
+        tt(a(o, 512 * ch, 512 * ch + 512), a(i, 512 * ch, 512 * ch + 512), a(rb("xT" if o == "Mc" else "zT", ch)), O.max)
 
     def gat(o, off, ch, more=(), lam=None):
         aff(a(o, 512 * ch, 512 * ch + 512), ind(a("P"), a(off, 32 * ch, 32 * ch + 32)), 1.0, 0.0, more, lam)
 
     def start(t):
         e = str(t % 2)
-        aff(a("xm" + e), ind(a("X"), a("vu" + e)), 1.0, -127.0)
         aff(a("Pv" + e), ind(a("P"), a("vu" + e)))
+        if t == 0 or not TM["xp"]:
+            aff(a("xm" + e), ind(a("X"), a("vu" + e)), 1.0, -127.0)
+        else:
+            aff(a("aY"), a("Pv" + e), 1.0, MAGIC)
+            aff(a("xm" + e), a("aY"), 1.0, c(22))
         it = []
         for h in range(2):
             it += [(half("M2", h), half("xm" + e, h), a("Ib")), (half("M2", h), a("onh", p=(0, 1)), a("offh", p=(0, 1)))]
@@ -360,7 +392,8 @@ def rank_program(g, core, T, topo):
         last = t == RO - 1
         K, e = "K%d" % t, str(t % 2)
         xm, Pv, vT, vb, aw = "xm" + e, "Pv" + e, a("vT" + e, 0, 16), "vb" + e, a("aw" + e)
-        cp(a("hc"), ind(a("B" if t == 0 else "L", 0, V), a("vu" + e)))
+        for lo, hi in ((0, 8), (8, 16)) if TM["hc"] else ((0, 16),):
+            cp(a("hc", 16 * lo, 16 * hi), ind(a("B" if t == 0 else "L", 0, V), a("vu" + e, lo, hi)))
         if t > 0:
             u = t - 1
             ts(a("LS%d" % u), ind(a("NL"), a("cu%d" % u, 0, 3)), float(V), O.add, float(MARK), O.min)
@@ -376,15 +409,18 @@ def rank_program(g, core, T, topo):
                 early(TM["xr"])
                 big("Mc", "Pc", ch)
             for k in range(16):
-                mm(k3(kb, None, 128 * h + k, 128 * h + 128, 16), lanes("Pc", h, k), a("W16c"), False, False)
-            for k in range(16):
-                mm(k3(kb, 0, 128 * h + k, 128 * h + 128, 16), lanes("Mc", h, k), a("b2"), False, k == 15)
+                mm(k3(kb, None, 128 * h + k, 128 * h + 128, 16), lanes("Pc", h, k), a("W16c"), False, k == 15)
             y, key = k3(kb, 1, 128 * h, 128 * h + 128), k3(kb, 0, 128 * h, 128 * h + 128)
-            act(half("aV", h), (y[0], y[1] + key[1]) + y[2:], F.Abs)
-            act(half("mv", h), half("aV", h), F.Relu, 4090.0, -SC)
-            tt(half("A", h), key, half("mv", h), O.add)
+            if h < TM["mw"]:
+                ts(half("mw", h), y, 0.0, O.is_equal, 4096.0, O.mult)
+            else:
+                act(half("aV", h), y, F.Abs)
+                act(half("mw", h), half("aV", h), F.Relu, 4096.0, -SC)
+            aff(half("mv", h), key)
+            y = k3("KO", 0, 128 * h, 128 * h + 128)
+            grp([(k3("KO", 0, 128 * h + k, 128 * h + 128, 16), lanes("Mc", h, k), a("b2")) for k in range(16)] + [(y, a("Ib"), half("mw", h))])
+            tt(half("A", h), y, half("mv", h), O.add)
             scan(half("sc", h), half("rst", h), half("A", h), 0.0, O.add, O.min)
-        act(a("mw"), a("aV"), F.Relu, 8192.0, -2 * SC)
         kmin = a("sc", 15, 256, 16)
         for h in range(2):
             lo, hi = 8 * h, 8 * h + 8
@@ -401,10 +437,10 @@ def rank_program(g, core, T, topo):
             ts(half("zT", h), z, MAGIC, O.add, MAGIC, O.subtract)
             early(TM["xh"] if h == 0 else 0.0)
         bT = a("bz", 0, 256, 16)
-        cp(bT, a("bI", 0, 16))
+        ts(bT, a("bI", 0, 16), -2048.0, O.add)
         aff(a(vb, 16, 32), a("M1", 0, 16))
-        grp([(half("M2", h), half("bz", h), a("I32m")) for h in range(2)])
-        aff(a("bR"), a("M2", 0, 256))
+        grp([(half("M2", h), half("bz", h), a("Ih")) for h in range(2)])
+        aff(a("bR"), a("M2", 0, 256), 1.0, 2048.0)
         sca(a("B"), a("sv" + e), a("bR"))
         ts(a("B16"), ind(a("B", 0, WN), a("bu")), -2048.0, O.add)
         rowlist("M1", 16, "B16", [(a("M1", 16, 32), a("I32m"), a("sl" + e))])
@@ -418,9 +454,9 @@ def rank_program(g, core, T, topo):
         aff(a("zr"), a("W", 256, 512), 1.0, c(10))
         it = []
         for h in range(2):
-            it += [(a("M1", 48 + 8 * h, 56 + 8 * h), half("Pb", h), a("W16c", 8, 16)), (a("M1", 48 + 8 * h, 56 + 8 * h), half(Pv, h), a("ns8"))]
+            it += [(a("M1", 32 + 16 * h, 48 + 16 * h), half(Pv, h), a("ns8")), (a("M1", 33 + 16 * h, 48 + 16 * h, 2), half("Pb", h), a("W16c", 8, 16))]
         for h in range(2):
-            it += [(a("M1", 32 + 8 * h, 40 + 8 * h), half(Pv, h), a("ns8")), (a("M1", 32 + 8 * h, 40 + 8 * h), half("Px", h), a("W16c", 8, 16))]
+            it += [(a("M1", 32 + 16 * h, 48 + 16 * h, 2), half("Px", h), a("W16c", 8, 16))]
         grp(it)
         n2 = 16 if last else 32
         if not last:
@@ -431,21 +467,17 @@ def rank_program(g, core, T, topo):
         tt(a("tmp", 64, 64 + n2), a("tmp", 0, n2), a("tmp", 32, 32 + n2), O.mult)
         add({"V": vts(m(13), m(4), 0.0, O.is_le, BIG, O.mult), "S": sact(m(13), m(4), F.Relu, BIG, -BIG)}, m(4)[1], m(13)[1])
         tt(m(14), bT, m(4), O.subtract)
-        aff(a("tv", 48, 64), m(14), 1.0 / 4096, 4081.5)
+        aff(a("tv", 48, 64), m(14), 1.0 / 4096, 4082.0)
         join = a("tj", 0, 16)
-        tt(join, a("M1", 32, 48), m(13), O.is_equal)
-        act(a("tw", 48, 64), a("M1", 48, 64), F.Abs)
+        tt(join, a("M1", 32, 64, 2), m(13), O.is_equal)
+        act(a("tw", 48, 64), a("M1", 33, 64, 2), F.Abs)
         aff(a("tw", 32, 48), kmin, SC, 8192.0)
         if not last:
             aff(m(15), m(2), -1.0, 1.0)
             tt(m(16), m(15), m(5), O.mult)
             tt(m(17), m(16), m(4), O.add)
-            aff(m(7), join, -1.0, 1.0)
-            tt(a("tj", 16, 32), m(7), m(17), O.mult)
-            conv("Yc", [(0, ("M1", 64, a("blkB"))), (0, ("M1", 80, a("blkB"))), (1, ("M1", 96, a("blk")))], a("tj"), 2,
-                 [(a("M1", 64, 96), a("I32m"), a("dum"))])
-        else:
-            conv("Yc", [(0, ("M1", 64, a("blkB"))), (0, ("M1", 80, a("blkB")))], join, 1, [(a("M1", 64, 96), a("I32m"), a("dum"))])
+            conv("Yc", [(0, ("M1", 96, a("blk")))], m(17), 1, [])
+        conv("Yj", [(0, ("M1", 64, a("blkB"))), (0, ("M1", 80, a("blkB")))], join, 1, [(a("M1", 64, 96), a("I32m"), a("dum"))])
         for x in range(4):
             aff(a("tq", 16 * x, 16 * x + 16), join, (-2 if x < 2 else 2) * BIG * SC, (1 if x < 2 else -1) * BIG * SC)
         tt(a("tz"), a("tq"), a("tw"), O.min)
@@ -465,7 +497,7 @@ def rank_program(g, core, T, topo):
             act(m(10), vT, F.Relu, 1.0 - GH)
             tt(a("tl"), join, m(10), O.is_gt)
             ts(a("vq"), vT, float(GH), O.subtract, 0.0, O.min)
-            ts(a("bq"), bT, float(GH), O.subtract, 0.0, O.min)
+            ts(a("bq"), bT, 2048.0 - GH, O.add, 0.0, O.min)
             grp([(a("M2", 0, 16), a("Tri"), a("tl")), (a("M2", 8, 16), a("onb"), a("tl", 0, 8))])
             grp([(a("W", 256, 512), a("I32m"), a(Pv)), (a("W", 256, 512), a("nIb"), a(xm)), (a("W", 256, 512), a("Ib"), a("zm"))])
             aff(a("PZ%d" % t, 0, 256), a("W", 256, 512))
@@ -497,14 +529,12 @@ def rank_program(g, core, T, topo):
         sca(a("X"), a(K, 0, 16), a("zr"))
         if last:
             dma(hb(T.yx[:]), a("X", 0, V), 256 * V)
-        mm(a("KZ", 0, 256), a("I32m"), a("A"), True, False)
-        for h in range(2):
-            for k in range(16):
-                mm(a("KZ", 128 * h + k, 128 * h + 128, 16), lanes("Mc", h, k), a("nb2"), False, False)
+            early(TM["yx"])
+        mm(a("KZ", 0, 256), a("I32m"), a("mv"), True, False)
         for h in range(2):
             mm(half("KZ", h), half(xm, h), a("pb"), False, False)
             mm(half("KZ", h), half("zm", h), a("nb"), False, False)
-        mm(a("KZ", 0, 256), a("Ib"), a("mw"), False, False)
+        mm(a("KZ", 0, 256), a("I2b"), a("mw"), False, False)
         for ch in range(8):
             gat("Po", "ho", ch)
         for x in range(16):
@@ -526,10 +556,15 @@ def rank_program(g, core, T, topo):
             aff(half("Ao", h), key)
             mm(a("KZ", 256 + 128 * h, 384 + 128 * h), a("I32m"), half("Ao", h), False, False)
             if h == 1:
-                tt(a("xo"), ind(a("tz", 48, 64), a("ru", 0, 16)), a("aY"), O.is_equal)
+                if TM["xo"]:
+                    for x in range(16):
+                        act(a("aV", 16 * x, 16 * x + 16), a("aY", 16 * x, 16 * x + 16), F.Abs, a("tz", 48 + x, 49 + x), -1.0)
+                    act(a("xw"), a("aV"), F.Relu, 8192.0, -2 * SC)
+                else:
+                    tt(a("xo"), ind(a("tz", 48, 64), a("ru", 0, 16)), a("aY"), O.is_equal)
                 mm(a("KZ", 0, 256), a("Ib"), a("gt"), False, False)
                 mm(a("KZ", 256, 512), a("Ib"), a("lt"), False, False)
-                mm(a("KZ", 256, 512), a("I8"), a("xo"), False, False)
+                mm(a("KZ", 256, 512), a("Ib" if TM["xo"] else "I8"), a("xw" if TM["xo"] else "xo"), False, False)
             for k in range(16):
                 mm(a("KZ", 128 * h + k, 128 * h + 128, 16), lanes("Mz", h, k), a("b2"), False, False)
             for k in range(16):
@@ -556,8 +591,7 @@ def rank_program(g, core, T, topo):
         aff(a("YF", x, x + 1280), a("Ft", x, x + 1280), 1.0, 1280.0, (), 0.0)
     for gg in range(8):
         dma(hb(T.yf[gg:gg + 1, :]), a("YF", p=(16 * gg, 16 * gg + 1)), 4 * V)
-
-    emit(g, T, ops)
+    return ops
 
 
 def _deps(ops, eng):
@@ -593,7 +627,39 @@ def _deps(ops, eng):
     return deps
 
 
-def _order(ops):
+def _replay(ops, deps, banks, order, eng, why=None):
+    wake = TM["wake"]
+    free = {q: 0.0 for q in "VSPGY"}
+    bank = {b: ("", -1e9, -1) for b in PSUM}
+    pipe, start, fin = 0.0, [0.0] * len(ops), [0.0] * len(ops)
+    before = {q: -1 for q in "VSPGY"}
+    for i in order:
+        q, kind = eng[i], ops[i][3]
+        s, w = (free[q], before[q]) if q else (0.0, -1)
+        for m in deps[i]:
+            if fin[m] + wake > s:
+                s, w = fin[m] + wake, m
+        for b in banks[i]:
+            if bank[b][0] != q and bank[b][1] + wake > s:
+                s, w = bank[b][1] + wake, bank[b][2]
+        if why is not None:
+            why[i] = w
+        before[q] = i
+        if kind == "c":
+            free[q] = fin[i] = s + ops[i][0][q][1]
+            for b in banks[i]:
+                bank[b] = (q, fin[i], i)
+        elif kind == "a":
+            fin[i] = s
+        else:
+            free[q] = s + 100.0
+            pipe = fin[i] = max(pipe, s + TM["dfix"]) + ops[i][0][q][1] / TM["bw"]
+    return fin
+
+
+def _order(every):
+    ops = every[0]
+    TM.update(CLOCKS[0])
     deps = _deps(ops, None)
     n = len(ops)
     wake = TM["wake"]
@@ -614,18 +680,94 @@ def _order(ops):
     banks = [set(r[0] for r in o[1] + o[2] if r[0] in PSUM) for o in ops]
     best = None
     rnd = np.random.RandomState(TM["seed"])
+    fixed = [None] * n
+    ends = [[m for m in sorted(deps[i]) if not (("P" in o[0] and "P" in ops[m][0]) or ("G" in o[0] and ops[m][3] == "r") or (
+        o[3] == "d" and ops[m][3] == "d" and not (o[1] and ops[m][2])))] for i, o in enumerate(ops)]
     for it in range(TM["it"]):
-        order, eng, fin = _greedy(ops, deps, succ, pri)
-        LOG.append(max(fin))
-        if best is None or max(fin) < best[0]:
-            best = (max(fin), order, eng, fin)
-        back = _pass(ops, succ, deps, banks, best[3], best[2])[1]
+        order, eng, fin = _greedy(ops, deps, succ, pri, fixed)
+        fins = []
+        for clock, other in zip(CLOCKS, every):
+            TM.update(clock)
+            fins.append(_replay(other, ends, banks, order, eng))
+        score = sum(max(f) / (clock["cy"] * (1.0 + clock["s"] / 8)) for f, clock in zip(fins, CLOCKS))
+        LOG.append(sum(max(f) for f in fins))
+        if best is None or score < best[0]:
+            best = (score, order, eng, fins)
+        k = int(rnd.randint(len(CLOCKS)))
+        TM.update(CLOCKS[k])
+        TM.update(look=float(rnd.choice(TM["looks"])), lamx=float(rnd.choice([0.2, 0.5, 1.0, 2.0])), lamy=float(rnd.choice([2.0, 4.0, 10.0])))
+        ops = every[k]
+        back = _pass(ops, succ, deps, banks, best[3][k], best[2])[1]
         noise = rnd.normal(0.0, TM["noise"] * min(it, 1), n)
-        pri = [TM["mix"] * back[i] + (1.0 - TM["mix"]) * (best[0] - best[3][i]) + float(noise[i]) for i in range(n)]
-    return best[1], best[2]
+        pri = [back[i] + float(noise[i]) for i in range(n)]
+        fixed = [None] * n
+        if it >= TM["whole"]:
+            place = [0] * n
+            for x, i in enumerate(best[1]):
+                place[i] = x
+            lo = int(rnd.randint(n))
+            inside = best[1][max(0, lo - TM["span"]):lo + TM["span"]]
+            for x, i in zip(sorted(place[i] for i in inside), sorted(inside, key=lambda i: -pri[i] - TM["more"] * float(noise[i]))):
+                place[i] = x
+            fixed = list(best[2])
+            for i in inside:
+                fixed[i] = None
+            pri = [-float(x) for x in place]
+    use = (0, 1, 4)
+
+    def judge(order, eng):
+        out, tot = [], 0.0
+        for k in use:
+            TM.update(CLOCKS[k])
+            why = [-1] * n
+            f = _replay(every[k], ends, banks, order, eng, why)
+            out.append((f, why))
+            tot += max(f) / (CLOCKS[k]["cy"] * (1.0 + CLOCKS[k]["s"] / 8))
+        return tot, out
+    order, eng = list(best[1]), list(best[2])
+    now, out = judge(order, eng)
+    top = (now, order, eng)
+    for it in range(TM["moves"]):
+        f, why = out[int(rnd.randint(len(use)))]
+        i = max(range(n), key=lambda x: f[x])
+        chain = []
+        while i >= 0:
+            if why[i] >= 0 and why[i] not in deps[i]:
+                chain.append(i)
+            i = why[i]
+        i = chain[int(rnd.randint(len(chain)))]
+        j = why[i]
+        o2, e2 = list(order), eng
+        pi, pj = o2.index(i), o2.index(j)
+        how = rnd.rand()
+        if len(ops[i][0]) > 1 and how < 0.5 or len(ops[j][0]) > 1 and how < 0.3:
+            x = i if len(ops[i][0]) > 1 else j
+            e2 = list(eng)
+            e2[x] = "V" if eng[x] == "S" else "S"
+        elif not deps[i].intersection(o2[pj:pi]):
+            o2.insert(pj, o2.pop(pi))
+        elif how > 0.6 and not set(succ[j]).intersection(o2[pj:pi + 1]):
+            o2.insert(pi, o2.pop(pj))
+        else:
+            take, want = [i], set(deps[i])
+            for x in o2[pi - 1:pj:-1]:
+                if x in want:
+                    take.append(x)
+                    want.update(deps[x])
+            if j in want:
+                continue
+            gone = set(take)
+            o2[pj:pi + 1] = take[::-1] + [x for x in o2[pj:pi + 1] if x not in gone]
+        new, out2 = judge(o2, e2)
+        if new < now + TM["heat"] * (1.0 - it / TM["moves"]) * rnd.rand():
+            now, out, order, eng = new, out2, o2, e2
+            if now < top[0]:
+                top = (now, order, eng)
+        LOG.append(top[0] * 2)
+    return top[1], top[2]
 
 
-def _greedy(ops, deps, succ, pri):
+def _greedy(ops, deps, succ, pri, fixed):
     n, wake = len(ops), TM["wake"]
     fin = [0.0] * n
     left = [len(d) for d in deps]
@@ -643,12 +785,16 @@ def _greedy(ops, deps, succ, pri):
             best = None
             if not ops[i][0]:
                 best = (rdy[i], rdy[i], None)
-            for q in ops[i][0]:
+            for q in [fixed[i]] if fixed[i] else ops[i][0]:
                 s = max(free[q], rdy[i])
                 for b in banks[i]:
                     if bank[b][0] != q:
                         s = max(s, bank[b][1] + wake)
                 lam = ops[i][0][q][2] if len(ops[i][0][q]) > 2 and ops[i][0][q][2] is not None else TM["lam"]
+                if lam == TM["lamc"]:
+                    lam = TM["lamx"]
+                elif lam > 0:
+                    lam = TM["lamy"]
                 key = s + ops[i][0][q][1] * ((1.0 + lam) if q == "V" else 1.0)
                 if best is None or key < best[0]:
                     best = (key, s, q)
@@ -794,10 +940,6 @@ PLAN = []
 
 def emit(g, T, ops):
     qs = {"V": g.vector, "S": g.scalar, "P": g.tensor, "G": g, "Y": g.sync}
-    if not PLAN:
-        order, eng = _order(ops)
-        eng = [eng[i] for i in order]
-        PLAN.extend([order, eng, _deps([ops[i] for i in order], eng)])
     order, eng, deps = PLAN
     ops = [ops[i] for i in order]
     strm = [eng[n] if o[3] == "c" else o[4] for n, o in enumerate(ops)]

import numpy as np
from concourse.mybir import AluOpType, ActivationFunctionType

V, GH, WN, LN, CAP, RO = 2560, 1536, 4096, 256, 48, 4
WD = 4416
MARK = 4096
ODUM = 4160
BIG = 1048576.0
MAGIC = 12582912.0
SC = 33554432.0
F32, BF, H16, I32, U16 = "float32", "bfloat16", "float16", "int32", "uint16"

SCRATCH = {}
PLACE = {}


def _sb(dtype, size, **kw):
    pool, at = "pool_" + dtype, 0
    for k in kw:
        if kw[k] > 64:
            SCRATCH[k] = ("sbuf", [128, kw[k]], dtype)
            PLACE[k] = (k, 0, kw[k], size)
        else:
            PLACE[k] = (pool, at, kw[k], size)
            at += (kw[k] + 15) // 16 * 16
    SCRATCH[pool] = ("sbuf", [128, at], dtype)


_sb(F32, 4, P=WD, L=WD, Ft=WD, Pc=4096, Po=4096, YF=V, Pv0=256, Pv1=256, Pb=256, Px=256, A=256, Ao=256, sc=256, aY=256, bR=256,
    Ya=256, Yb=256, Yc=512, rp=256, aV=256, mv=256, t1=256, t2=256, tv=64, tj=32, vb0=32, vb1=32, tmp=512, tc=384, acc0=32, acc1=32,
    bia0=32, bia1=32, vT0=32, vT1=32, aw0=16, aw1=16, sl0=16, sl1=16, tw=64, tq=64, tz=64, s1=16, l0f=16,
    I32m=128, nsr=128, W16c=16, W16o=16, ns8=16, blk=8, mR=512, rst=256, rs8=48, Gm=48, I384=384, col=32, LNc=16, dum=32,
    ds=8, thf=8, on32=128, lnf=16, g24=24, gs=48, gs2=48, gs3=8, gs4=8, LM0=48, LM1=48, LM2=48, DT0=304, DT1=304, DT2=304,
    PZ0=312, PZ1=312, PZ2=312, EM0=56, EM1=56, EM2=56, LS0=48, LS1=48, LS2=48)
_sb(BF, 2, X=WD, xm0=256, xm1=256, xb=256, zr=256, zm=256, gt=256, lt=256, mw=256, xw=256, Yj=256, blkB=8, junk=4352, Ib=128, nIb=128, hIb=128, I2b=128, pb=128, nb=128, IO=512, WI=128,
    Tri=128, onb=128, tl=16)
_sb(H16, 2, Mc=4096, Mo=4096, Mz=4096, xT=256, zT=256, xo=256, bz=256, p160=256, p161=256, B16=256, OH=768, Ih=128,
    I8=128, Rep=512, b2=8, nb2=8, s0=8, Big=144, onh=128, offh=128, j5=256, ph=128, Y0=256, vq=16, bq=16, lnh=2)
_sb(I32, 4, B=WD, NL=256, ki=256, kb=16, kc=16, bI=32, JI=256, J2=256, J3=512, pI=8, l0=16, thi=8)
_sb(U16, 2, hc=256, ho=256, vu0=16, vu1=16, bu=16, sv0=16, sv1=16, xu=16, tu=16, ru=64, ou=24, cu0=4, cu1=4, cu2=4,
    K0=40, K1=40, K2=40, K3=40)
for _n in ("R0", "R1", "KZ", "M1", "M2", "W"):
    SCRATCH[_n] = ("psum", [128, 512], F32)
    PLACE[_n] = (_n, 0, 512, 4)
for _n in ("KC", "KO"):
    SCRATCH[_n] = ("psum", [128, 2, 256], F32)
PSUM = ("R0", "R1", "KZ", "M1", "M2", "W", "KC", "KO")
SEMAPHORES = ["eV", "eS", "eP", "eG"] + ["d%d" % i for i in range(24)] + ["r%d" % i for i in range(8)] + ["l%d" % i for i in range(8)]

TM = dict(cy=1.04, g=1.56, s=3.8, pe=0.53, fix=60.0, wake=100.0, bw=200.0, dfix=2000.0, look=150.0, lam=4.0, lamc=0.5, sg=8, xa=20000.0,
          xr=1000.0, xz=0.0, xt=0.0, k1="KC", xh=35000.0, xo=0, xp=1, mw=1, hc=0, r3=1, whole=999, span=150, more=3.0, moves=8000, heat=100.0, lamx=0.5, lamy=4.0, gv=1536, yx=0.0, it=40, seed=1, noise=30.0, looks=[60.0, 100.0, 150.0, 220.0])


CLOCKS = [dict(cy=0.83, pe=0.42, g=1.56, s=3.8, fix=30.0, wake=50.0, bw=250.0), dict(cy=0.9, pe=0.45, g=1.2, s=2.2, fix=40.0, wake=60.0, bw=250.0),
          dict(cy=1.04, pe=0.52, g=1.56, s=3.8, fix=40.0, wake=70.0, bw=200.0), dict(cy=1.2, pe=0.6, g=1.9, s=5.0, fix=40.0, wake=60.0, bw=250.0),
          dict(cy=1.1, pe=0.55, g=1.6, s=4.0, fix=50.0, wake=170.0, bw=130.0)]
for _c in CLOCKS:
    _c["dfix"] = 3200.0 if _c["bw"] < 150 else 2000.0


def rank_program(g, core, T, topo):
    if T.rank_of(core) is None:
        return
    if not PLAN:
        every = []
        for clock in CLOCKS:
            TM.update(clock)
            every.append(calls(g, core, T, topo))
        order, eng = _order(every)
        eng = [eng[i] for i in order]
        PLAN.extend([order, eng, _deps([every[0][i] for i in order], eng)])
    emit(g, T, calls(g, core, T, topo))


def calls(g, core, T, topo):
    rank = T.rank_of(core)
    O, F = AluOpType, ActivationFunctionType
    dst = T.cores[(rank - 1) % len(T.cores)]
    rid, pid = topo.addr(dst)[0], topo.addr(dst)[1]
    emask = topo.mask(core, dst)
    neng = len(topo.engines(core, dst))
    ops = []

    def a(n, lo=0, hi=None, st=None, p=None):
        buf, at, w, size = PLACE[n]
        if hi is None:
            hi = w
        ps = slice(None) if p is None else slice(p[0], p[1])
        return (T[buf][ps, slice(at + lo, at + hi, st)], [(n, lo, hi)], len(range(lo, hi, st or 1)), size, n in PSUM, False)

    def k3(n, r, lo, hi, st=None):
        rr = (0, 1) if r is None else (r,)
        return (T[n][:, slice(None) if r is None else r, slice(lo, hi, st)], [(n, 256 * x + lo, 256 * x + hi) for x in rr],
                len(rr) * len(range(lo, hi, st or 1)), 4, True, False)

    def ind(w, o):
        return (w[0].indirect(o[0]), w[1] + o[1], 16 * o[2], w[3], False, True)

    def val(x):
        return x[0] if isinstance(x, tuple) else x

    def rs(*xs):
        return [r for x in xs if isinstance(x, tuple) for r in x[1]]

    def add(alts, rd, wr, kind="c", sem=None, n=1):
        ops.append((alts, rd, wr, kind, sem, n, [0.0]))

    def early(x):
        ops[-1][6][0] = x

    def tm(n, per):
        return TM["fix"] + max(64.0, n * per) * TM["cy"]

    def one(o, x):
        return tm(o[2], TM["g"] if x[5] else 0.5 if o[3] == 2 and x[3] == 2 else 1.0)

    def cp(o, i):
        add({"V": (lambda: g.vector.tensor_copy(o[0], i[0]), one(o, i))}, i[1], o[1])

    def sca(w, off, i):
        add({"V": (lambda: g.vector.tensor_copy(w[0].indirect(off[0]), i[0]), tm(i[2], TM["s"]))}, i[1] + off[1], w[1])

    def tt(o, x, y, op):
        add({"V": (lambda: g.vector.tensor_tensor(o[0], x[0], y[0], op), tm(o[2], TM["g"] if x[5] else 1.0 if x[4] or y[4] else 2.0))},
            x[1] + y[1], o[1])

    def vts(o, x, s1, op0, s2=None, op1=None):
        if op1 is None:
            return (lambda: g.vector.tensor_scalar(o[0], x[0], val(s1), None, op0), one(o, x))
        return (lambda: g.vector.tensor_scalar(o[0], x[0], val(s1), val(s2), op0, op1), one(o, x))

    def ts(o, x, s1, op0, s2=None, op1=None):
        add({"V": vts(o, x, s1, op0, s2, op1)}, rs(x, s1, s2), o[1])

    def scan(o, d0, d1, init, op0, op1):
        add({"V": (lambda: g.vector.tensor_tensor_scan(o[0], d0[0], d1[0], init, op0, op1), tm(o[2], 1.0))}, d0[1] + d1[1], o[1])

    def ms(o, c):
        add({"V": (lambda: g.vector.memset(o[0], c), one(o, o))}, [], o[1])

    def sact(o, i, f, bias, scale):
        return (lambda: g.scalar.activation(o[0], i[0], f, bias=val(bias), scale=val(scale)), tm(o[2], TM["g"] if i[5] else 1.0))

    def act(o, i, f=F.Identity, bias=0.0, scale=1.0, acc=None):
        if acc is None:
            add({"S": sact(o, i, f, bias, scale)}, rs(i, bias, scale), o[1])
        else:
            add({"S": (lambda: g.scalar.activation(o[0], i[0], f, bias=val(bias), scale=val(scale), accum_out=acc[0]), tm(o[2], 1.0) + 20)},
                rs(i, bias, scale), o[1] + acc[1])

    def aff(o, x, scale=1.0, bias=0.0, more=(), lam=None):
        add({"V": vts(o, x, scale, O.mult, bias, O.add) + (lam,), "S": sact(o, x, F.Identity, bias, scale)}, rs(x, scale, bias) + list(more), o[1])

    def mm(o, l, r, st, sp):
        add({"P": (lambda: g.tensor.matmul(o[0], l[0], r[0], st, sp), 10 + max(min(64, l[2]), r[2]) * (4 if l[3] == 4 else 1) * TM["pe"])},
            l[1] + r[1], o[1])

    def grp(items):
        for n, (o, l, r) in enumerate(items):
            if n == len(items) - 1:
                o = (o[0], [x for it in items for x in it[0][1]]) + o[2:]
            mm(o, l, r, n == 0, n == len(items) - 1)

    def iota(o, pat, base, cm, fl=True):
        if fl:
            add({"G": (lambda: g.iota(o[0], pat, base, cm, allow_small_or_imprecise_dtypes=True), 130 + 2 * o[2] * TM["cy"])}, [], o[1])
        else:
            add({"G": (lambda: g.iota(o[0], pat, base, cm), 130 + 2 * o[2] * TM["cy"])}, [], o[1])

    nd, nr = [0], [0]

    def dma(o, i, size):
        add({"Y": (lambda: g.sync.dma_start(o[0], i[0]), size)}, i[1], o[1], "d", "d%d" % nd[0], 16)
        nd[0] += 1

    def send(o, i, more=()):
        n = nr[0]
        nr[0] += 1
        add({"G": (lambda: g.remote_dma(o[0], i[0], T.sem["r%d" % n], T.sem["l%d" % n], pid, rid, emask), 128 * i[2] * i[3])},
            i[1] + list(more), [], "r", "l%d" % n, neng)
        add({}, [], o[1], "a", "r%d" % n, neng)

    def hb(x):
        return (x, [])

    dma(a("X", 0, GH), hb(T.feat[:, 0:GH]), 256 * GH)
    dma(a("l0"), hb(T.lane0[:]), 8192)
    dma(a("X", GH, V), hb(T.feat[:, GH:V]), 256 * (V - GH))
    dma(a("B", 0, 768), hb(T.hits[:, 0:768]), 512 * 768)
    for lo, hi in ((768, GH), (GH, 2048), (2048, V)):
        dma(a("B", lo, hi), (T.hits[:, lo:hi], [("X", GH, V)] if lo == 768 else []), 512 * (hi - lo))
    dma(a("thi", p=(0, 1)), hb(T.th[:]), 32)


    iota(a("pI", 0, 1), [[0, 1]], 0, 1, False)
    iota(a("JI"), [[1, 256]], 0, 0, False)
    iota(a("J2"), [[0, 16], [1, 16]], 0, 0, False)
    iota(a("IO", p=(0, 32)), [[1, 8], [0, 64]], 0, 0)
    iota(a("IO", p=(32, 64)), [[0, 8], [1, 64]], 0, 0)
    send(a("X", V, WN), a("X", 0, GH))
    iota(a("J3"), [[1, 32], [0, 16]], 0, 0, False)
    iota(a("g24"), [[0, 3], [1, 8]], 0, 0)
    iota(a("I384"), [[16, 3], [0, 8], [1, 16]], 1, 0)
    for x in range(0, WD, 552):
        iota(a("Ft", x, x + 552), [[1, 552]], x - 1280, 0)
    iota(a("B", V, 3488), [[0, 928]], 0, 0, False)
    iota(a("B", 3488, WD), [[0, 928]], 0, 0, False)
    for o in ops:
        if "G" in o[0]:
            o[2].append(("~", 0, 1))

    def c(n):
        return a("col", n, n + 1)
    ts(a("pI", 1, 2), a("pI", 0, 1), 15, O.bitwise_and)
    ts(a("pI", 2, 3), a("pI", 0, 1), 31, O.bitwise_and)
    ts(a("pI", 3, 4), a("pI", 0, 1), 4, O.logical_shift_right)
    cp(a("col", 0, 4), a("pI", 0, 4))
    ts(a("col", 4, 7), a("JI", 0, 3), c(1), O.is_equal)
    ts(c(7), c(1), 2.0, O.is_lt)
    ts(c(8), c(4), 1224.0, O.mult, -124.0, O.add)
    ts(c(9), c(5), -1280.0, O.mult, c(8), O.add)
    aff(c(10), c(9), -1.0)
    aff(c(11), c(9), -1.0, -127.0)
    aff(c(22), c(11), 1.0, -MAGIC)
    aff(c(12), c(4), -0.625)
    ts(c(13), c(0), 16.0, O.add, c(4), O.mult)
    ts(c(14), c(4), 2016.0 / 4096, O.mult, c(9), O.add)
    ts(c(15), c(5), 32.0 / 4096, O.mult, c(14), O.add)
    ts(c(16), c(4), -0.125, O.mult)
    ts(a("col", 24, 32), a("JI", 0, 8), c(16), O.mult, c(15), O.add)
    ts(a("Ib"), a("JI", 0, 128), c(0), O.is_equal)
    ts(a("mR", 0, 256), a("J2"), c(1), O.is_equal)
    aff(a("mR", 256, 512), a("mR", 0, 256))
    ts(c(17), c(0), 0.0, O.is_equal, -1.0 / 64, O.mult)
    ts(c(18), c(0), 32.0, O.is_equal, -1.0 / 4096, O.mult)
    ts(c(19), c(0), 32.0, O.is_equal)
    tt(c(20), c(17), c(18), O.add)
    ts(a("WI"), a("J2", 0, 128), c(19), O.is_equal, c(20), O.mult)
    ts(a("rst"), a("J2", 0, 256), 0.0, O.is_equal, BIG, O.mult)
    ts(a("tc", 0, 128), a("J2", 0, 128), 0.0, O.is_equal, 1224.0, O.mult)
    ts(a("tc", 128, 256), a("J2", 0, 128), 1.0, O.is_equal, -1280.0, O.mult)
    tt(a("tc", 256, 384), a("tc", 0, 128), a("tc", 128, 256), O.add)
    ts(a("offh"), a("tc", 256, 384), 3.0, O.add)
    ts(a("ph"), a("J3", 0, 128), c(3), O.is_equal)
    ts(a("Ih"), a("JI", 0, 128), c(0), O.is_equal)
    ts(a("onh"), a("JI", 0, 128), 0.0, O.is_ge)
    ts(a("j5"), a("JI", 0, 256), 1.0 / 512, O.mult)
    cp(a("ru"), a("JI", 0, 64))
    ts(a("blk"), a("JI", 0, 8), c(3), O.is_equal)
    ts(a("s0"), a("blk"), c(4), O.mult)
    ts(a("LNc"), a("JI", 0, 16), 16.0, O.mult, c(1), O.add)
    aff(a("lnf"), a("LNc"), 1.0 / 512)
    ts(a("Rep"), a("J3"), c(2), O.is_equal)
    ts(a("pb"), a("J3", 0, 128), c(3), O.is_equal)
    aff(a("nb"), a("pb"), -1.0)
    ts(a("nsr"), a("pb"), c(7), O.mult, -1.0, O.mult)
    aff(a("I32m"), a("Ib"))
    ts(a("b2"), a("blk"), 2.0, O.mult)
    aff(a("I2b"), a("Ib"), 4.0)
    aff(a("W16c", 0, 8), a("blk"), -1.0)
    aff(a("W16o", 0, 8), a("blk"), -1.0)
    aff(a("W16c", 8, 16), a("blk"), c(7))
    aff(a("W16o", 8, 16), a("W16c", 8, 16), 2.0)
    aff(a("ns8", 0, 16, 2), a("W16c", 8, 16), -1.0)
    aff(a("ns8", 1, 16, 2), a("W16c", 8, 16), -1.0)
    ms(a("P", WN, WD), 0.0)
    aff(c(21), c(4), 5000.0)
    aff(a("P", MARK, MARK + 1), c(6), -30000.0, c(21))
    ms(a("X", WN, WD), 0.0)
    ms(a("L", WN, WD), 0.0)
    ts(a("bz"), a("JI"), 0.0, O.mult)
    aff(a("nIb"), a("Ib"), -1.0)
    aff(a("hIb"), a("Ib"), 0.5)
    ts(a("I8"), a("Ib"), 8192.0, O.mult)
    aff(a("blkB"), a("blk"), -BIG)
    ts(a("Big"), a("JI", 1, 145), c(13), O.is_equal)
    ts(a("Tri"), a("JI", 0, 128), c(0), O.is_ge)
    aff(a("onb"), a("Ib"), 0.0, 1.0)
    aff(a("on32"), a("Ib"), 0.0, 1.0)
    aff(a("dum", 0, 16), a("LNc"), 1.0, float(ODUM))
    aff(a("dum", 16, 32), a("LNc"), 1.0, float(ODUM))
    aff(a("ds", 0, 3), a("LNc", 0, 3), 1.0, 16.0)
    aff(a("ds", 3, 6), a("LNc", 0, 3), 1.0, 16.0)
    ts(a("lnh", 0, 1), c(0), 1.0, O.mult)
    ts(a("lnh", 1, 2), c(0), 128.0, O.add)
    cp(a("ou"), a("g24"))
    ts(a("Gm", 0, 24), a("g24"), c(3), O.is_equal)
    aff(a("Gm", 24, 48), a("Gm", 0, 24))
    ts(a("rs8", 0, 24), a("g24"), 0.0, O.is_gt)
    aff(a("rs8", 24, 48), a("rs8", 0, 24))

    def half(n, h):
        return a(n, 128 * h, 128 * h + 128)

    def lanes(n, h, k):
        return a(n, 2048 * h + k, 2048 * h + 2048, 16)

    def places(t, lm):
        e = str(t % 2)
        ts(a("vu" + e), lm, 1280.0, O.add)
        aff(a("bia" + e, 0, 16), lm, -1.0, 1.0 / 1024)
        aff(a("vb" + e, 0, 16), lm, 1.0, 1280.0)
        tt(a("bia" + e, 16, 32), a("bia" + e, 0, 16), a("lnf"), O.subtract)
        grp([(a("W", 0, 256), a("Ih"), a("p16" + e)), (a("W", 0, 256), a("onh", p=(0, 1)), a("j5", p=(0, 1)))])
        grp([(a("M1", 128 + 8 * h, 136 + 8 * h), half("p16" + e, h), a("s0")) for h in range(2)])
        aff(a("vT" + e, 0, 16), a("M1", 128, 144), 1.0, 1280.0)
        aff(a("vT" + e, 16, 32), a("M1", 128, 144), 1.0, 1280.0)
        at = 0
        for q in range(16):
            for s in range(2):
                act(a("junk", at, at + 16 * q + 16), a("W", 0, 16 * q + 16), F.Sign, a("bia" + e, 16 * s + q, 16 * s + q + 1), 1.0,
                    a("acc" + e, 16 * s + q, 16 * s + q + 1))
                at += 16 * q + 16

    def conv(y, out, src, n, extra):
        tt(a(y, 0, 256 * n), ind(src, a("ru", 0, 16 * n)), a("mR", 0, 256 * n), O.mult)
        it = []
        for j, o in out:
            it += [((a(o[0], o[1] + 8 * h, o[1] + 8 * h + 8)), a(y, 256 * j + 128 * h, 256 * j + 128 * h + 128), o[2]) for h in range(2)]
        grp(extra + it)

    def rowlist(bank, lo, src, extra=()):
        grp(list(extra) + [(a(bank, lo, lo + 16), a("Big", 15 - r, 143 - r), a(src, r, 256, 16)) for r in range(16)])

    def m(n):
        return a("tmp", 16 * n, 16 * n + 16)

    def awake(t):
        e = str(t % 2)
        tt(m(20), a("acc" + e, 0, 16), a("acc" + e, 16, 32), O.subtract)
        early(TM["xa"] if t else 0.0)
        aff(a("sl" + e), m(20), 4096.0)
        grp([(a("M1", 144, 160), a("I32m"), a("vb" + e, 0, 16)), (a("M1", 144, 160), a("I32m"), a("sl" + e))])
        tt(m(23), a("M1", 144, 160), a("dum", 0, 16), O.min)
        cp(a("sv" + e), m(23))
        act(a("aw" + e), m(20), F.Relu, 1.0, -1.0)

    ts(a("l0f"), a("l0"), -1280.0, O.add)
    tt(a("Y0"), ind(a("l0f"), a("ru", 0, 16)), a("mR", 0, 256), O.mult)
    grp([(a("M2", 0, 256), a("ph"), a("Y0"))])
    cp(a("p160"), a("M2", 0, 256))
    places(0, a("l0f"))
    for ch in range(8):
        r = a("R%d" % (ch % 2))
        grp([(r, a("Ib"), a("X", 512 * ch, 512 * ch + 512)), (r, a("WI", p=(0, 64)), a("IO", p=(0, 64)))])
        aff(a("P", 512 * ch, 512 * ch + 512), r, 1.0, c(24 + ch))
    ts(a("thf", p=(0, 1)), a("thi", p=(0, 1)), -7.5, O.add)
    for lo, hi in ((0, 384), (384, 768), (768, 1152), (1152, GH), (GH, 2048), (2048, V)):
        cp(a("L", lo, hi), a("B", lo, hi))
    for x in range(0, GH, 384):
        if x < TM["gv"]:
            ts(a("Po", GH + x, GH + x + 384), a("B", x, x + 384), float(V), O.add, float(MARK), O.min)
        else:
            act(a("Po", x, x + 384), a("L", x, x + 384), F.Relu, float(GH), -1.0)
            act(a("Po", GH + x, GH + x + 384), a("Po", x, x + 384), F.Identity, float(MARK), -1.0)
    send(a("L", V, WN), a("Po", GH, 2 * GH), [("B", GH, V)])

    def rep(src, ch):
        h, cc = divmod(ch, 4)
        grp([(a(rb(src, ch)), a(src, 128 * h, 128 * h + 128, p=(32 * cc, 32 * cc + 32)), a("Rep", p=(32 * cc, 32 * cc + 32)))])

    def rb(src, ch):
        return ("R0", "R1", "KZ")[ch % 3] if src == "xT" and TM["r3"] else "R%d" % (ch % 2)

    def big(o, i, ch):
        tt(a(o, 512 * ch, 512 * ch + 512), a(i, 512 * ch, 512 * ch + 512), a(rb("xT" if o == "Mc" else "zT", ch)), O.max)

    def gat(o, off, ch, more=(), lam=None):
        aff(a(o, 512 * ch, 512 * ch + 512), ind(a("P"), a(off, 32 * ch, 32 * ch + 32)), 1.0, 0.0, more, lam)

    def start(t):
        e = str(t % 2)
        aff(a("Pv" + e), ind(a("P"), a("vu" + e)))
        if t == 0 or not TM["xp"]:
            aff(a("xm" + e), ind(a("X"), a("vu" + e)), 1.0, -127.0)
        else:
            aff(a("aY"), a("Pv" + e), 1.0, MAGIC)
            aff(a("xm" + e), a("aY"), 1.0, c(22))
        it = []
        for h in range(2):
            it += [(half("M2", h), half("xm" + e, h), a("Ib")), (half("M2", h), a("onh", p=(0, 1)), a("offh", p=(0, 1)))]
        grp(it)
        cp(a("xT"), a("M2", 0, 256))
        early(TM["xt"] if t else 0.0)

    start(0)
    grp([(a("M2", 336 + 8 * h, 344 + 8 * h), a("on32", p=(0, 1)), a("thf", p=(0, 1))) for h in range(2)])
    aff(a("tw", 0, 16), a("M2", 336, 352), -SC, 8192.0)
    aff(a("tw", 16, 32), a("M2", 336, 352), SC)
    awake(0)
    for t in range(RO):
        last = t == RO - 1
        K, e = "K%d" % t, str(t % 2)
        xm, Pv, vT, vb, aw = "xm" + e, "Pv" + e, a("vT" + e, 0, 16), "vb" + e, a("aw" + e)
        for lo, hi in ((0, 8), (8, 16)) if TM["hc"] else ((0, 16),):
            cp(a("hc", 16 * lo, 16 * hi), ind(a("B" if t == 0 else "L", 0, V), a("vu" + e, lo, hi)))
        if t > 0:
            u = t - 1
            ts(a("LS%d" % u), ind(a("NL"), a("cu%d" % u, 0, 3)), float(V), O.add, float(MARK), O.min)
            send(a("LM%d" % u), a("LS%d" % u))
            sca(a("L", V, WD), a("K%d" % u, 16, 19), a("LM%d" % u)) if False else sca(a("L"), a("K%d" % u, 16, 19), a("LM%d" % u))
        for h in range(2):
            kb = "KC" if h == 0 else TM["k1"]
            mm(k3(kb, 0, 128 * h, 128 * h + 128), half(xm, h), a("nb"), True, False)
            mm(k3(kb, 1, 128 * h, 128 * h + 128), half(Pv, h), a("nsr"), False, False)
            for ch in range(4 * h, 4 * h + 4):
                gat("Pc", "hc", ch, [("acc" + e, 0, 32)] if t > 0 and ch >= TM["sg"] else [], TM["lamc"])
                rep("xT", ch)
                early(TM["xr"])
                big("Mc", "Pc", ch)
            for k in range(16):
                mm(k3(kb, None, 128 * h + k, 128 * h + 128, 16), lanes("Pc", h, k), a("W16c"), False, k == 15)
            y, key = k3(kb, 1, 128 * h, 128 * h + 128), k3(kb, 0, 128 * h, 128 * h + 128)
            if h < TM["mw"]:
                ts(half("mw", h), y, 0.0, O.is_equal, 4096.0, O.mult)
            else:
                act(half("aV", h), y, F.Abs)
                act(half("mw", h), half("aV", h), F.Relu, 4096.0, -SC)
            aff(half("mv", h), key)
            y = k3("KO", 0, 128 * h, 128 * h + 128)
            grp([(k3("KO", 0, 128 * h + k, 128 * h + 128, 16), lanes("Mc", h, k), a("b2")) for k in range(16)] + [(y, a("Ib"), half("mw", h))])
            tt(half("A", h), y, half("mv", h), O.add)
            scan(half("sc", h), half("rst", h), half("A", h), 0.0, O.add, O.min)
        kmin = a("sc", 15, 256, 16)
        for h in range(2):
            lo, hi = 8 * h, 8 * h + 8
            ts(a("kb", lo, hi), a("sc", 128 * h + 15, 128 * h + 128, 16), 4096.0, O.mult, 2048.0, O.add)
            ts(a("bI", lo, hi), a("kb", lo, hi), 4095, O.bitwise_and)
            tt(half("Yb", h), ind(a("bI", lo, hi), a("ru", 0, 8)), a("mR", 0, 128), O.mult)
            grp([(a("M1", lo, hi), half("Yb", h), a("blk"))])
            cp(a("bu", lo, hi), a("M1", lo, hi))
            aff(half("xb", h), ind(a("X"), a("bu", lo, hi)), 1.0, -127.5)
            cp(half("ho", h), ind(a("L", 0, WN), a("bu", lo, hi)))
            early(TM["xh"] if h == 0 else 0.0)
            z = a("M2", 256 + 128 * h, 384 + 128 * h)
            grp([(z, half(xm, h), a("hIb")), (z, a("onh", p=(0, 1)), a("offh", p=(0, 1))), (z, half("xb", h), a("hIb"))])
            ts(half("zT", h), z, MAGIC, O.add, MAGIC, O.subtract)
            early(TM["xh"] if h == 0 else 0.0)
        bT = a("bz", 0, 256, 16)
        ts(bT, a("bI", 0, 16), -2048.0, O.add)
        aff(a(vb, 16, 32), a("M1", 0, 16))
        grp([(half("M2", h), half("bz", h), a("Ih")) for h in range(2)])
        aff(a("bR"), a("M2", 0, 256), 1.0, 2048.0)
        sca(a("B"), a("sv" + e), a("bR"))
        ts(a("B16"), ind(a("B", 0, WN), a("bu")), -2048.0, O.add)
        rowlist("M1", 16, "B16", [(a("M1", 16, 32), a("I32m"), a("sl" + e))])
        ts(a("xu"), a("M1", 16, 32), 2048.0, O.add, float(MARK), O.min)
        aff(a("Px"), ind(a("P"), a("xu")))
        aff(a("Pb"), ind(a("P"), a("bu")))
        for h in range(2):
            z = a("W", 256 + 128 * h, 384 + 128 * h)
            grp([(z, half("zT", h), a("Ih"))])
            aff(half("zm", h), z, 1.0, c(11))
        aff(a("zr"), a("W", 256, 512), 1.0, c(10))
        it = []
        for h in range(2):
            it += [(a("M1", 32 + 16 * h, 48 + 16 * h), half(Pv, h), a("ns8")), (a("M1", 33 + 16 * h, 48 + 16 * h, 2), half("Pb", h), a("W16c", 8, 16))]
        for h in range(2):
            it += [(a("M1", 32 + 16 * h, 48 + 16 * h, 2), half("Px", h), a("W16c", 8, 16))]
        grp(it)
        n2 = 16 if last else 32
        if not last:
            ts(a("kc"), a("A", t, 256, 16), 4096.0, O.mult, 2048.0, O.add)
            ts(a("bI", 16, 32), a("kc"), 4095, O.bitwise_and)
        tt(a("tmp", 0, n2), a("bI", 0, n2), a("vT" + e, 0, n2), O.subtract)
        ts(a("tmp", 32, 32 + n2), a("bI", 0, n2), float(V), O.is_lt)
        tt(a("tmp", 64, 64 + n2), a("tmp", 0, n2), a("tmp", 32, 32 + n2), O.mult)
        add({"V": vts(m(13), m(4), 0.0, O.is_le, BIG, O.mult), "S": sact(m(13), m(4), F.Relu, BIG, -BIG)}, m(4)[1], m(13)[1])
        tt(m(14), bT, m(4), O.subtract)
        aff(a("tv", 48, 64), m(14), 1.0 / 4096, 4082.0)
        join = a("tj", 0, 16)
        tt(join, a("M1", 32, 64, 2), m(13), O.is_equal)
        act(a("tw", 48, 64), a("M1", 33, 64, 2), F.Abs)
        aff(a("tw", 32, 48), kmin, SC, 8192.0)
        if not last:
            aff(m(15), m(2), -1.0, 1.0)
            tt(m(16), m(15), m(5), O.mult)
            tt(m(17), m(16), m(4), O.add)
            conv("Yc", [(0, ("M1", 96, a("blk")))], m(17), 1, [])
        conv("Yj", [(0, ("M1", 64, a("blkB"))), (0, ("M1", 80, a("blkB")))], join, 1, [(a("M1", 64, 96), a("I32m"), a("dum"))])
        for x in range(4):
            aff(a("tq", 16 * x, 16 * x + 16), join, (-2 if x < 2 else 2) * BIG * SC, (1 if x < 2 else -1) * BIG * SC)
        tt(a("tz"), a("tq"), a("tw"), O.min)
        tt(a("tv", 0, 16), a("tz", 0, 16), a("tz", 32, 48), O.max)
        aff(a("tv", 16, 32), join, -2 * SC, SC)
        act(a("rp"), ind(a("tv", 48, 64), a("ru", 0, 16)))
        tt(a("tmp", 176, 208), a("M1", 64, 96), a(vb), O.max)
        cp(a(K, 20, 36), a("tmp", 192, 208))
        cp(a(K, 0, 16), a("tmp", 176, 192))
        sca(a("Ft"), a(K, 20, 36), a("p16" + e))
        if not last:
            tt(m(6), a("M1", 96, 112), aw, O.mult)
            tt(m(8), m(6), a(vb, 0, 16), O.add)
            cp(a("tu"), m(8))
            cp(a("p16" + str((t + 1) % 2)), ind(a("Ft", 0, V), a("tu")))
            rowlist("M1", 112, "p16" + str((t + 1) % 2))
            act(m(10), vT, F.Relu, 1.0 - GH)
            tt(a("tl"), join, m(10), O.is_gt)
            ts(a("vq"), vT, float(GH), O.subtract, 0.0, O.min)
            ts(a("bq"), bT, 2048.0 - GH, O.add, 0.0, O.min)
            grp([(a("M2", 0, 16), a("Tri"), a("tl")), (a("M2", 8, 16), a("onb"), a("tl", 0, 8))])
            grp([(a("W", 256, 512), a("I32m"), a(Pv)), (a("W", 256, 512), a("nIb"), a(xm)), (a("W", 256, 512), a("Ib"), a("zm"))])
            aff(a("PZ%d" % t, 0, 256), a("W", 256, 512))
            tt(a("s1"), a("M2", 0, 16), a("tl"), O.mult)
            for h in range(2):
                tt(a("OH", 384 * h, 384 * h + 384), ind(a("s1", 8 * h, 8 * h + 8), a("ou")), a("I384"), O.is_equal)
            it = []
            for q in range(3):
                for h in range(2):
                    oh = a("OH", 384 * h + 128 * q, 384 * h + 128 * q + 128)
                    it += [(a("M2", 16 + 8 * q, 24 + 8 * q), oh, a("vq", 8 * h, 8 * h + 8)), (a("M2", 40 + 8 * q, 48 + 8 * q), oh, a("bq", 8 * h, 8 * h + 8)),
                           (a("M2", 64 + q, 65 + q), oh, a("lnh", h, h + 1))]
            grp(it)
            cp(a("cu%d" % t, 0, 3), a("M2", 64, 67))
            tt(a("gs"), a("M2", 16, 64), a("Gm"), O.mult)
            scan(a("gs2"), a("rs8"), a("gs"), 0.0, O.mult, O.add)
            sums = a("gs2", 7, 48, 8)
            ts(a("gs3", 0, 6), sums, 0.0, O.is_ge)
            tt(a("gs4", 0, 6), a("gs3", 0, 6), a("ds", 0, 6), O.mult)
            tt(a("EM%d" % t, 48, 54), a("gs4", 0, 6), sums, O.add)
            aff(a("EM%d" % t, 0, 48), ind(a("PZ%d" % t, 0, 256), a("cu%d" % t, 0, 3)), 1.0, c(12))
            send(a("PZ%d" % t, 256, 310), a("EM%d" % t, 0, 54))
            places(t + 1, a("M1", 112, 128))
            awake(t + 1)
        else:
            for u in (2, 1, 0):
                aff(a("DT%d" % u, 0, 256), ind(a("Ft"), a("K%d" % u, 0, 16)))
                sca(a("Ft"), a("K%d" % u, 20, 36), a("DT%d" % u, 0, 256))
        sca(a("X"), a(K, 0, 16), a("zr"))
        if last:
            dma(hb(T.yx[:]), a("X", 0, V), 256 * V)
            early(TM["yx"])
        mm(a("KZ", 0, 256), a("I32m"), a("mv"), True, False)
        for h in range(2):
            mm(half("KZ", h), half(xm, h), a("pb"), False, False)
            mm(half("KZ", h), half("zm", h), a("nb"), False, False)
        mm(a("KZ", 0, 256), a("I2b"), a("mw"), False, False)
        for ch in range(8):
            gat("Po", "ho", ch)
        for x in range(16):
            act(a("gt", 16 * x, 16 * x + 16), a("A", 16 * x, 16 * x + 16), F.Relu, a("tv", x, x + 1), a("tv", 16 + x, 17 + x))
            act(a("lt", 16 * x, 16 * x + 16), a("A", 16 * x, 16 * x + 16), F.Relu, a("tz", 16 + x, 17 + x), -SC)
        for h in range(2):
            y, key = k3("KO", 1, 128 * h, 128 * h + 128), k3("KO", 0, 128 * h, 128 * h + 128)
            mm(y, half(Pv, h), a("nsr"), True, False)
            mm(y, half("Pb", h), a("nsr"), False, False)
            mm(key, half("zm", h), a("nb"), False, False)
            for ch in range(4 * h, 4 * h + 4):
                rep("zT", ch)
                early(TM["xz"])
                big("Mz", "Pc", ch)
                big("Mo", "Po", ch)
            for k in range(16):
                mm(k3("KO", None, 128 * h + k, 128 * h + 128, 16), lanes("Po", h, k), a("W16o"), False, k == 15)
            act(half("aY", h), y, F.Abs)
            aff(half("Ao", h), key)
            mm(a("KZ", 256 + 128 * h, 384 + 128 * h), a("I32m"), half("Ao", h), False, False)
            if h == 1:
                if TM["xo"]:
                    for x in range(16):
                        act(a("aV", 16 * x, 16 * x + 16), a("aY", 16 * x, 16 * x + 16), F.Abs, a("tz", 48 + x, 49 + x), -1.0)
                    act(a("xw"), a("aV"), F.Relu, 8192.0, -2 * SC)
                else:
                    tt(a("xo"), ind(a("tz", 48, 64), a("ru", 0, 16)), a("aY"), O.is_equal)
                mm(a("KZ", 0, 256), a("Ib"), a("gt"), False, False)
                mm(a("KZ", 256, 512), a("Ib"), a("lt"), False, False)
                mm(a("KZ", 256, 512), a("Ib" if TM["xo"] else "I8"), a("xw" if TM["xo"] else "xo"), False, False)
            for k in range(16):
                mm(a("KZ", 128 * h + k, 128 * h + 128, 16), lanes("Mz", h, k), a("b2"), False, False)
            for k in range(16):
                mm(a("KZ", 256 + 128 * h + k, 384 + 128 * h, 16), lanes("Mo", h, k), a("b2"), False, h == 1 and k == 15)
        kz = a("KZ", 0, 256)
        tt(a("t1"), (kz[0], [("KZ", 0, 512)]) + kz[2:], a("rp"), O.min)
        tt(a("t2"), a("KZ", 256, 512), a("t1"), O.min)
        grp([(half("M2", h), half("t2", h), a("I32m")) for h in range(2)])
        ts(a("ki"), a("M2", 0, 256), 4096.0, O.mult, 2048.0, O.add)
        ts(a("NL"), a("ki"), 4095, O.bitwise_and)
        sca(a("L"), a("sv" + e), a("NL"))
        if not last:
            pz = "PZ%d" % t
            ts(a(K, 16, 19), a(pz, 304, 307), float(WN), O.add)
            ts(a(K, 36, 39), a(pz, 307, 310), float(WN), O.add)
            sca(a("P"), a(K, 0, 19), a(pz, 0, 304))
            sca(a("P"), a(K, 20, 39), a(pz, 0, 304))
            for u in range(t - 1, -1, -1):
                aff(a("DT%d" % u), ind(a("P"), a("K%d" % u, 0, 19)))
                sca(a("P"), a("K%d" % u, 20, 39), a("DT%d" % u))
            start(t + 1)
    dma(hb(T.yl[:]), a("L", 0, V), 512 * V)
    for x in range(0, V, 1280):
        aff(a("YF", x, x + 1280), a("Ft", x, x + 1280), 1.0, 1280.0, (), 0.0)
    for gg in range(8):
        dma(hb(T.yf[gg:gg + 1, :]), a("YF", p=(16 * gg, 16 * gg + 1)), 4 * V)
    return ops


def _deps(ops, eng):
    acc, deps, lastg, lasty = {}, [], [], []
    for n, (alts, rd, wr, kind, sem, cnt, _x) in enumerate(ops):
        d = set()
        pe = "P" in alts
        use = [(r, False) for r in rd] + [(r, True) for r in wr if eng is None or r[0] != "~"]
        for (name, lo, hi), w in use:
            ps = name in PSUM
            for (m, w2, lo2, hi2) in acc.get(name, []):
                if pe and ps and "P" in ops[m][0]:
                    if eng is None:
                        d.add(m)
                elif (lo < hi2 and lo2 < hi and (w or w2)) or (ps and eng is not None and eng[m] != eng[n]):
                    d.add(m)
        if eng is not None and eng[n] == "G" and kind == "c":
            d.update(lastg)
            lastg[:] = [n]
        if eng is None and kind == "a":
            d.add(n - 1)
        if eng is None and kind == "d":
            d.update(lasty)
            lasty[:] = [n]
        for (name, lo, hi), w in use:
            lst = acc.setdefault(name, [])
            if w and name not in PSUM:
                lst[:] = [x for x in lst if not (lo <= x[2] and x[3] <= hi)]
            elif name in PSUM and len(lst) > 200:
                del lst[:50]
            lst.append((n, w, lo, hi))
        deps.append(d)
    return deps


def _replay(ops, deps, banks, order, eng, why=None):
    wake = TM["wake"]
    free = {q: 0.0 for q in "VSPGY"}
    bank = {b: ("", -1e9, -1) for b in PSUM}
    pipe, start, fin = 0.0, [0.0] * len(ops), [0.0] * len(ops)
    before = {q: -1 for q in "VSPGY"}
    for i in order:
        q, kind = eng[i], ops[i][3]
        s, w = (free[q], before[q]) if q else (0.0, -1)
        for m in deps[i]:
            if fin[m] + wake > s:
                s, w = fin[m] + wake, m
        for b in banks[i]:
            if bank[b][0] != q and bank[b][1] + wake > s:
                s, w = bank[b][1] + wake, bank[b][2]
        if why is not None:
            why[i] = w
        before[q] = i
        if kind == "c":
            free[q] = fin[i] = s + ops[i][0][q][1]
            for b in banks[i]:
                bank[b] = (q, fin[i], i)
        elif kind == "a":
            fin[i] = s
        else:
            free[q] = s + 100.0
            pipe = fin[i] = max(pipe, s + TM["dfix"]) + ops[i][0][q][1] / TM["bw"]
    return fin


def _order(every):
    ops = every[0]
    TM.update(CLOCKS[0])
    deps = _deps(ops, None)
    n = len(ops)
    wake = TM["wake"]

    def least(i):
        o = ops[i]
        if o[3] == "a":
            return 0.0
        x = min(v[1] for v in o[0].values())
        return x if o[3] == "c" else TM["dfix"] + x / TM["bw"] if o[2] or o[3] == "r" or i >= n - 11 else 100.0
    succ = [[] for _ in range(n)]
    for i in range(n):
        for m in deps[i]:
            succ[m].append(i)
    pri = [0.0] * n
    for i in range(n - 1, -1, -1):
        pri[i] = least(i) + ops[i][6][0] + max([pri[j] + (0.0 if "P" in ops[i][0] and "P" in ops[j][0] else wake) for j in succ[i]] + [0.0])
    banks = [set(r[0] for r in o[1] + o[2] if r[0] in PSUM) for o in ops]
    best = None
    rnd = np.random.RandomState(TM["seed"])
    fixed = [None] * n
    ends = [[m for m in sorted(deps[i]) if not (("P" in o[0] and "P" in ops[m][0]) or ("G" in o[0] and ops[m][3] == "r") or (
        o[3] == "d" and ops[m][3] == "d" and not (o[1] and ops[m][2])))] for i, o in enumerate(ops)]
    for it in range(TM["it"]):
        order, eng, fin = _greedy(ops, deps, succ, pri, fixed)
        fins = []
        for clock, other in zip(CLOCKS, every):
            TM.update(clock)
            fins.append(_replay(other, ends, banks, order, eng))
        score = sum(max(f) / (clock["cy"] * (1.0 + clock["s"] / 8)) for f, clock in zip(fins, CLOCKS))
        LOG.append(sum(max(f) for f in fins))
        if best is None or score < best[0]:
            best = (score, order, eng, fins)
        k = int(rnd.randint(len(CLOCKS)))
        TM.update(CLOCKS[k])
        TM.update(look=float(rnd.choice(TM["looks"])), lamx=float(rnd.choice([0.2, 0.5, 1.0, 2.0])), lamy=float(rnd.choice([2.0, 4.0, 10.0])))
        ops = every[k]
        back = _pass(ops, succ, deps, banks, best[3][k], best[2])[1]
        noise = rnd.normal(0.0, TM["noise"] * min(it, 1), n)
        pri = [back[i] + float(noise[i]) for i in range(n)]
        fixed = [None] * n
        if it >= TM["whole"]:
            place = [0] * n
            for x, i in enumerate(best[1]):
                place[i] = x
            lo = int(rnd.randint(n))
            inside = best[1][max(0, lo - TM["span"]):lo + TM["span"]]
            for x, i in zip(sorted(place[i] for i in inside), sorted(inside, key=lambda i: -pri[i] - TM["more"] * float(noise[i]))):
                place[i] = x
            fixed = list(best[2])
            for i in inside:
                fixed[i] = None
            pri = [-float(x) for x in place]
    use = (0, 1, 4)

    def judge(order, eng):
        out, tot = [], 0.0
        for k in use:
            TM.update(CLOCKS[k])
            why = [-1] * n
            f = _replay(every[k], ends, banks, order, eng, why)
            out.append((f, why))
            tot += max(f) / (CLOCKS[k]["cy"] * (1.0 + CLOCKS[k]["s"] / 8))
        return tot, out
    order, eng = list(best[1]), list(best[2])
    now, out = judge(order, eng)
    top = (now, order, eng)
    for it in range(TM["moves"]):
        f, why = out[int(rnd.randint(len(use)))]
        i = max(range(n), key=lambda x: f[x])
        chain = []
        while i >= 0:
            if why[i] >= 0 and why[i] not in deps[i]:
                chain.append(i)
            i = why[i]
        i = chain[int(rnd.randint(len(chain)))]
        j = why[i]
        o2, e2 = list(order), eng
        pi, pj = o2.index(i), o2.index(j)
        how = rnd.rand()
        if len(ops[i][0]) > 1 and how < 0.5 or len(ops[j][0]) > 1 and how < 0.3:
            x = i if len(ops[i][0]) > 1 else j
            e2 = list(eng)
            e2[x] = "V" if eng[x] == "S" else "S"
        elif not deps[i].intersection(o2[pj:pi]):
            o2.insert(pj, o2.pop(pi))
        elif how > 0.6 and not set(succ[j]).intersection(o2[pj:pi + 1]):
            o2.insert(pi, o2.pop(pj))
        else:
            take, want = [i], set(deps[i])
            for x in o2[pi - 1:pj:-1]:
                if x in want:
                    take.append(x)
                    want.update(deps[x])
            if j in want:
                continue
            gone = set(take)
            o2[pj:pi + 1] = take[::-1] + [x for x in o2[pj:pi + 1] if x not in gone]
        new, out2 = judge(o2, e2)
        if new < now + TM["heat"] * (1.0 - it / TM["moves"]) * rnd.rand():
            now, out, order, eng = new, out2, o2, e2
            if now < top[0]:
                top = (now, order, eng)
        LOG.append(top[0] * 2)
    return top[1], top[2]


def _greedy(ops, deps, succ, pri, fixed):
    n, wake = len(ops), TM["wake"]
    fin = [0.0] * n
    left = [len(d) for d in deps]
    rdy = [0.0] * n
    ready = [i for i in range(n) if left[i] == 0]
    free = {q: 0.0 for q in "VSPGY"}
    bank = {b: ("", 0.0) for b in PSUM}
    banks = [set(r[0] for r in o[1] + o[2] if r[0] in PSUM) for o in ops]
    pipe = [0.0]
    start, eng = [0.0] * n, [None] * n
    order = []
    while ready:
        cand = []
        for i in ready:
            best = None
            if not ops[i][0]:
                best = (rdy[i], rdy[i], None)
            for q in [fixed[i]] if fixed[i] else ops[i][0]:
                s = max(free[q], rdy[i])
                for b in banks[i]:
                    if bank[b][0] != q:
                        s = max(s, bank[b][1] + wake)
                lam = ops[i][0][q][2] if len(ops[i][0][q]) > 2 and ops[i][0][q][2] is not None else TM["lam"]
                if lam == TM["lamc"]:
                    lam = TM["lamx"]
                elif lam > 0:
                    lam = TM["lamy"]
                key = s + ops[i][0][q][1] * ((1.0 + lam) if q == "V" else 1.0)
                if best is None or key < best[0]:
                    best = (key, s, q)
            cand.append((best[1], i, best[2]))
        lo = min(x[0] for x in cand)
        s, i, q = max((x for x in cand if x[0] <= lo + TM["look"]), key=lambda x: (pri[x[1]], -x[1]))
        ready.remove(i)
        order.append(i)
        start[i], eng[i] = s, q
        if ops[i][3] == "c":
            end = s + ops[i][0][q][1]
            free[q] = end
            for b in banks[i]:
                bank[b] = (q, end)
        elif ops[i][3] == "a":
            end = s
        else:
            free[q] = s + 100.0
            pipe[0] = max(pipe[0], s + TM["dfix"]) + ops[i][0][q][1] / TM["bw"]
            end = pipe[0]
        fin[i] = end
        for j in succ[i]:
            after = s if (ops[i][3] == "d" and ops[j][3] == "d" and not (ops[j][1] and ops[i][2])) or (q == "P" and "P" in ops[j][0]) or (
                ops[i][3] == "r" and "G" in ops[j][0]) else end + wake
            rdy[j] = max(rdy[j], after)
            left[j] -= 1
            if left[j] == 0:
                ready.append(j)
    return order, eng, fin


def _gap(busy, t, c, pad):
    lo, hi = 0, len(busy)
    while lo < hi:
        mid = (lo + hi) // 2
        if busy[mid][1] + pad <= t:
            lo = mid + 1
        else:
            hi = mid
    while lo < len(busy) and busy[lo][0] < t + c + pad:
        t = max(t, busy[lo][1] + pad)
        lo += 1
    return t


def _put(busy, s, e):
    lo, hi = 0, len(busy)
    while lo < hi:
        mid = (lo + hi) // 2
        if busy[mid][0] < s:
            lo = mid + 1
        else:
            hi = mid
    busy.insert(lo, (s, e))


def _pass(ops, pred, succ, banks, pri, fixed):
    n, wake = len(ops), TM["wake"]
    left = [len(d) for d in pred]
    ready = [i for i in range(n) if left[i] == 0]
    busy = {q: [] for q in "VSPGYD"}
    bank = {b: {q: [] for q in "VSP"} for b in PSUM}
    start, end, eng = [0.0] * n, [0.0] * n, [None] * n
    while ready:
        i = max(ready, key=lambda x: pri[x])
        ready.remove(i)
        alts, kind = ops[i][0], ops[i][3]
        r = 0.0
        for m in pred[i]:
            if kind == "d" and ops[m][3] == "d" and not (ops[max(i, m)][1] and ops[min(i, m)][2]):
                x = start[m]
            elif "G" in alts and "G" in ops[m][0] and ops[min(i, m)][3] == "r":
                x = start[m]
            elif "P" in alts and "P" in ops[m][0]:
                x = end[m]
            else:
                x = end[m] + wake
            if x > r:
                r = x
        best = (r, r, None, r)
        for z, q in enumerate([fixed[i]] if fixed and alts else alts):
            c = alts[q][1] if kind == "c" else 100.0
            s = r
            while True:
                s0 = s
                s = _gap(busy[q], s, c, 0.0)
                for b in banks[i]:
                    for o in "VSP":
                        if o != q:
                            s = _gap(bank[b][o], s, c, wake)
                if s == s0:
                    break
            lam = alts[q][2] if len(alts[q]) > 2 and alts[q][2] is not None else TM["lam"]
            key = s + c * ((1.0 + lam) if q == "V" else 1.0)
            if z == 0 or key < best[0]:
                best = (key, s, q, s + c)
        s, q, e = best[1:]
        if q is not None:
            _put(busy[q], s, e)
            for b in banks[i]:
                _put(bank[b][q], s, e)
            if kind != "c":
                c = alts[q][1] / TM["bw"]
                d = s + TM["dfix"] if fixed else _gap(busy["D"], s + TM["dfix"], c, 0.0)
                _put(busy["D"], d, d + c)
                e = d + c
        start[i], end[i], eng[i] = s, e, q
        for j in succ[i]:
            left[j] -= 1
            if left[j] == 0:
                ready.append(j)
    return start, end, eng


def _order2(ops):
    n = len(ops)
    pred = [sorted(d) for d in _deps(ops, None)]
    succ = [[] for _ in range(n)]
    for i in range(n):
        for m in pred[i]:
            succ[m].append(i)
    banks = [set(r[0] for r in o[1] + o[2] if r[0] in PSUM) for o in ops]
    pri = [0.0] * n
    for i in range(n - 1, -1, -1):
        o = ops[i]
        x = min([v[1] for v in o[0].values()] + [1e9]) if o[0] else 0.0
        x = x if o[3] in "ca" else TM["dfix"] + x / TM["bw"]
        pri[i] = x + o[6][0] + max([pri[j] + TM["wake"] for j in succ[i]] + [0.0])
    best = None
    for it in range(TM["it"]):
        start, end, eng = _pass(ops, pred, succ, banks, pri, None)
        if best is None or max(end) < best[0]:
            best = (max(end), start, eng)
        LOG.append(max(end))
        bs, be, _ = _pass(ops, succ, pred, banks, end, eng)
        pri = be
    return sorted(range(n), key=lambda i: (best[1][i], i)), best[2]


LOG = []
PLAN = []


def emit(g, T, ops):
    qs = {"V": g.vector, "S": g.scalar, "P": g.tensor, "G": g, "Y": g.sync}
    order, eng, deps = PLAN
    ops = [ops[i] for i in order]
    strm = [eng[n] if o[3] == "c" else o[4] for n, o in enumerate(ops)]
    known = {q: {} for q in qs}
    after, waits = [], []
    for n, o in enumerate(ops):
        w, vc = [], {}
        if eng[n] is not None:
            kn = known[eng[n]]
            for m in sorted(deps[n], reverse=True):
                if kn.get(strm[m], -1) < m:
                    w.append(m)
                    for s in after[m]:
                        if kn.get(s, -1) < after[m][s]:
                            kn[s] = after[m][s]
            vc = dict(kn)
        vc[strm[n]] = n
        after.append(vc)
        waits.append(w)
    need = set(m for w in waits for m in w)
    count, at = {}, {}
    for n, o in enumerate(ops):
        if o[3] != "c":
            at[n] = (o[4], o[5])
        elif n in need:
            count[eng[n]] = count.get(eng[n], 0) + 1
            at[n] = ("e" + eng[n], count[eng[n]])
    for n, o in enumerate(ops):
        if eng[n] is None:
            continue
        for m in waits[n]:
            qs[eng[n]].wait_ge(T.sem[at[m][0]], at[m][1])
        ins = o[0][eng[n]][0]()
        if o[3] == "d":
            ins.then_inc(T.sem[o[4]], 16)
        elif o[3] == "c" and n in need:
            ins.then_inc(T.sem[at[n][0]], 1)
    for n, o in enumerate(ops):
        if o[3] != "c" and n not in need:
            g.wait_ge(T.sem[at[n][0]], at[n][1])
